import numpy as np
import ml_dtypes


def mxq(x, axis, fmt="e4m3"):
    dtype, down = {"e4m3": (ml_dtypes.float8_e4m3fn, 7), "e5m2": (ml_dtypes.float8_e5m2, 14)}[fmt]
    v = np.moveaxis(np.asarray(x, np.float32).astype(ml_dtypes.bfloat16).astype(np.float64), axis, -1)
    blocks = v.reshape(v.shape[:-1] + (-1, 32))
    amax = np.abs(blocks).max(-1, keepdims=True)
    byte = np.maximum(np.where(amax > 0, np.frexp(amax)[1] - 1 + 127, 0) - down, 1)
    scale = np.exp2(byte - 127.0)
    codes = (blocks / scale).astype(np.float32).astype(dtype).astype(np.float64)
    return np.moveaxis((codes * scale).reshape(v.shape), -1, axis)


WIDE = False


def mx_kscale(k):
    if not WIDE:
        return np.ones(k)
    levels = np.array([10, -10, 5, -5, 0])
    if k % 512:
        return np.exp2(np.random.permutation(np.resize(levels, k // 32))).repeat(32)
    a = np.empty((k // 512, 16))
    for p in range(k // 512):
        a[p, :8] = np.random.permutation(np.resize(levels, 8))
        for g in range(8):
            far = levels[np.abs(levels - a[p, g]) >= 10]
            a[p, g + 8] = far[np.random.randint(len(far))]
    return np.exp2(a.ravel()).repeat(32)


def f64(x):
    return np.asarray(x).astype(np.float64)


def striped(idx):
    return np.tile(idx.reshape(-1, 16).T, (8, 1)).astype(np.uint16)


def unstriped(offs):
    return offs[:16].T.reshape(-1).astype(np.int64)


def pack_weight(w):
    k, n = w.shape
    w = f64(np.asarray(w, np.float32).astype(ml_dtypes.bfloat16)).reshape(k // 32, 32, n)
    amax = np.abs(w).max(1)
    byte = np.clip(np.where(amax > 0, np.frexp(amax)[1] - 1 + 127 - 7, 1), 1, 254)
    scaled = (w * np.exp2(127.0 - byte)[:, None, :]).reshape(k, n).astype(np.float32)
    words = np.ascontiguousarray(scaled.reshape(k // 512, 128, 4, n).transpose(0, 1, 3, 2)).astype(ml_dtypes.float8_e4m3fn).view(np.uint8)
    return words, np.ascontiguousarray(byte.astype(np.uint8).reshape(k // 512, 16, n))


def unpack_weight(words, scales):
    g, p, n, _ = words.shape
    vals = np.ascontiguousarray(words).view(ml_dtypes.float8_e4m3fn).astype(np.float64) * np.repeat(np.exp2(scales.astype(np.float64) - 127.0), 8, axis=1)[..., None]
    return vals.transpose(0, 1, 3, 2).reshape(g * 512, n)


def gelu(v):
    return 0.5 * v * (1.0 + np.tanh(np.sqrt(2.0 / np.pi) * (v + 0.044715 * v**3)))


K, T, D, H, N = 512, 1024, 2, 512, 128
P = 2 ** 7


def setup_inputs():
    n = np.random.standard_normal
    s = mx_kscale(K)[:, None]
    u = mx_kscale(H)
    packed_xT = pack_weight(n((K, T)) * s)
    packed_w2 = pack_weight(n((H, N)) / np.sqrt(H) / u[:, None])
    return {
        "x_words": packed_xT[0],
        "x_scales": packed_xT[1],
        "w1": (n((K, H)) / np.sqrt(K) / s * u).astype(np.float32),
        "w2_words": packed_w2[0],
        "w2_scales": packed_w2[1],
        "gate": (np.tile(np.random.uniform(0.2, 1.0, (D, 1, T)) / np.sqrt(D), (1, P, 1))).astype(np.float32),
        "pos1": striped(np.random.permutation(T)),
        "pos2": striped(np.random.permutation(T)),
    }


def reference(x_words, x_scales, w1, w2_words, w2_scales, gate, pos1, pos2):
    xq = unpack_weight(x_words, x_scales)
    h = gelu(mxq(f64(w1), 0, "e4m3").T @ xq)
    z = h - (h[:, unstriped(pos1)] * f64(gate)[0, :1] + h[:, unstriped(pos2)] * f64(gate)[1, :1])
    return unpack_weight(w2_words, w2_scales).T @ mxq(z, 0, "e4m3")

@@ -1,0 +1,196 @@
+from contextlib import ExitStack
+
+import concourse.mybir as mybir
+from concourse.masks import make_identity
+
+K, T, H, N = 512, 1024, 512, 128
+FLOPS = 2 * K * H * T + 2 * H * N * T
+
+F32 = mybir.dt.float32
+BF16 = mybir.dt.bfloat16
+I32 = mybir.dt.int32
+U32 = mybir.dt.uint32
+U16 = mybir.dt.uint16
+U8 = mybir.dt.uint8
+FP8X4 = mybir.dt.float8_e4m3fn_x4
+ACT = mybir.ActivationFunctionType
+MULT = mybir.AluOpType.mult
+
+P = 128
+BANK = 512
+CHUNKS = (512, 384, 128)
+
+
+def load_scale_rows(queue, plane, rows):
+    for q in range(4):
+        queue.dma_start(out=plane[32 * q : 32 * q + 4, :].bitcast(I32), in_=rows[4 * q : 4 * q + 4, :].bitcast(I32))
+
+
+def mx_pieces(n):
+    pieces, at = [], 0
+    for width in (512, 256, 128):
+        if n - at >= width:
+            pieces.append((at, width))
+            at = at + width
+    return pieces
+
+
+def tile_picked_wlapl_gelu_l_kernel(
+    tc, x_words, x_scales, w1, w2_words, w2_scales, gate, pos1, pos2, out
+):
+    nc = tc.nc
+    with ExitStack() as ctx:
+        keep = ctx.enter_context(tc.tile_pool(name="keep", bufs=1))
+        ring = ctx.enter_context(tc.tile_pool(name="ring", bufs=1))
+        psum = ctx.enter_context(tc.psum_pool(name="psum", bufs=1))
+
+        x_plane = keep.tile([P, T], U8, align_bytes=64)
+        w2_plane = keep.tile([P, N], U8, align_bytes=64)
+        nc.vector.memset(x_plane[:].bitcast(I32), 0)
+        warm = keep.tile([P, 2], F32)
+        nc.vector.memset(warm[:, 0:1], 0.0)
+        nc.vector.memset(w2_plane[:].bitcast(I32), 0)
+
+        w1_rows = w1.rearrange("(p j) c -> p j c", j=4)
+        w_raw = [keep.tile([P, 4, P], F32, name=f"w_raw{c}") for c in range(4)]
+        x_codes = [keep.tile([P, BANK], U32, name=f"x_codes{s}", align_bytes=64) for s in range(2)]
+        x_bytes = x_words[0].rearrange("p n t -> p (n t)")
+        gate_cols = keep.tile([P, 2, 8], F32)
+        lists = [keep.tile([P, T // 16], U16, name=f"list{d}") for d in range(2)]
+        w2_codes = keep.tile([P, N], U32, align_bytes=64)
+
+        nc.sync.dma_start(out=w_raw[0][:], in_=w1_rows[:, :, 0:P])
+        nc.sync.dma_start(out=x_codes[0][:].bitcast(I32), in_=x_bytes[:, 0 : 4 * BANK].bitcast(I32))
+        load_scale_rows(nc.scalar, x_plane, x_scales[0])
+        nc.sync.dma_start(out=gate_cols[:], in_=gate[:, 0, :].rearrange("d (n j) -> n d j", j=8))
+        nc.sync.dma_start(out=x_codes[1][:].bitcast(I32), in_=x_bytes[:, 4 * BANK : 8 * BANK].bitcast(I32))
+        nc.sync.dma_start(out=w_raw[1][:], in_=w1_rows[:, :, P : 2 * P])
+        nc.sync.dma_start(lists[0][:], pos1)
+        nc.sync.dma_start(lists[1][:], pos2)
+        for c in (2, 3):
+            nc.sync.dma_start(out=w_raw[c][:], in_=w1_rows[:, :, c * P : (c + 1) * P])
+        nc.sync.dma_start(out=w2_codes[:].bitcast(I32), in_=w2_words[0].rearrange("p n t -> p (n t)").bitcast(I32))
+        load_scale_rows(nc.sync, w2_plane, w2_scales[0])
+
+        nc.scalar.activation(out=warm[:, 1:2], in_=warm[:, 0:1], func=ACT.Gelu_apprx_tanh)
+        ident = keep.tile([P, P], F32)
+        make_identity(nc, ident[:])
+
+        minus_gate = [keep.tile([P, T], F32, name=f"minus_gate{d}") for d in range(2)]
+        for d in range(2):
+            for half in range(2):
+                spread = psum.tile([P, 4, P], F32, name="spread", tag="sum", bufs=5)
+                for j in range(4):
+                    col = 4 * half + j
+                    nc.tensor.transpose(spread[:, j, :], gate_cols[:, d, col : col + 1].to_broadcast([P, P]), ident[:])
+                nc.scalar.activation(
+                    out=minus_gate[d][:].rearrange("q (n h j) -> q h n j", h=2, j=4)[:, half],
+                    in_=spread[:].rearrange("q j n -> q n j"),
+                    func=ACT.Copy,
+                    scale=-1.0,
+                )
+
+        w_codes, w_planes = [], []
+        w_bf = []
+        for c in range(4):
+            bf = keep.tile([P, P, 4], BF16, name=f"w_bf{c}", align_bytes=64)
+            nc.vector.tensor_copy(
+                out=bf[:].rearrange("p (m i) j -> p m j i", i=4),
+                in_=w_raw[c][:].rearrange("p j (m i) -> p m j i", i=4),
+            )
+            codes = keep.tile([P, P], U32, name=f"w_codes{c}", align_bytes=64)
+            plane = keep.tile([P, P], U8, name=f"w_plane{c}", align_bytes=64)
+            nc.vector.quantize_mx(
+                out=codes[:].bitcast(FP8X4), scales=plane[:], in_=bf[:].rearrange("p m j -> p (m j)")
+            )
+            w_codes.append(codes)
+            w_planes.append(plane)
+
+        h = [keep.tile([P, T], F32, name=f"h{c}") for c in range(4)]
+        for c in range(4):
+            for s in range(2):
+                cols = slice(s * BANK, (s + 1) * BANK)
+                pre = psum.tile([P, BANK], F32, name="pre", tag="pair", bufs=2)
+                nc.tensor.matmul_mx(
+                    out=pre[:],
+                    lhsT=w_codes[c][:].bitcast(FP8X4),
+                    lhsT_scale=w_planes[c][:],
+                    rhs=x_codes[s][:].bitcast(FP8X4),
+                    rhs_scale=x_plane[:, cols],
+                    start=True,
+                    stop=True,
+                )
+                nc.scalar.activation(out=h[c][:, cols], in_=pre[:], func=ACT.Gelu_apprx_tanh)
+
+        v0 = 0
+        for ci, n in enumerate(CHUNKS):
+            last = ci == len(CHUNKS) - 1
+            blocks = n // P
+            sums = [psum.tile([P, H], F32, name="sums", tag="sum", bufs=5) for b in range(blocks)]
+            for c in range(4):
+                terms = []
+                for d in range(2):
+                    term = ring.tile([P, n], F32, name="term", tag="term", bufs=8)
+                    nc.vector.tensor_tensor(
+                        term[:],
+                        h[c][:].indirect(lists[d][:, v0 // 16 : (v0 + n) // 16]),
+                        minus_gate[d][:, v0 : v0 + n],
+                        MULT,
+                    )
+                    terms.append(term)
+                for b in range(blocks):
+                    parts = [h[c][:, v0 + b * P : v0 + (b + 1) * P]] + [t[:, b * P : (b + 1) * P] for t in terms]
+                    for i, part in enumerate(parts):
+                        nc.tensor.matmul(
+                            sums[b][:, c * P : (c + 1) * P],
+                            lhsT=part,
+                            rhs=ident[:],
+                            start=(i == 0),
+                            stop=(i == 2),
+                            is_transpose=True,
+                        )
+
+            z_bf = ring.tile([P, n, 4], BF16, name="z_bf", tag="z_bf", bufs=3, align_bytes=64)
+            z_words = z_bf[:].rearrange("p v t -> p (v t)").bitcast(F32)
+            for b0 in range(0, blocks, 2):
+                nb = min(2, blocks - b0)
+                back = psum.tile([P, nb, 2, P], F32, name="back", tag="pair", bufs=2)
+                for b in range(b0, b0 + nb):
+                    z_rows = ring.tile([P, H], BF16, name="z_rows", tag="z_rows", bufs=3)
+                    nc.scalar.copy(
+                        out=z_rows[:].rearrange("v (u p e) -> v u p e", u=2, e=2),
+                        in_=sums[b][:].rearrange("v (p u e) -> v u p e", u=2, e=2),
+                    )
+                    pairs = z_rows[:].bitcast(F32)
+                    for u in range(2):
+                        nc.tensor.transpose(back[:, b - b0, u, :], pairs[:, u * P : (u + 1) * P], ident[:])
+                nc.scalar.copy(
+                    out=z_words[:, 2 * P * b0 : 2 * P * (b0 + nb)].rearrange("p (b v u) -> p b v u", b=nb, u=2),
+                    in_=back[:].rearrange("p b u v -> p b v u"),
+                )
+
+            for at, width in mx_pieces(n):
+                z_codes = ring.tile([P, width], U32, name="z_codes", tag="z_codes", bufs=4, align_bytes=64)
+                z_plane = ring.tile([P, width], U8, name="z_plane", tag="z_plane", bufs=4, align_bytes=64)
+                nc.vector.quantize_mx(
+                    out=z_codes[:].bitcast(FP8X4),
+                    scales=z_plane[:],
+                    in_=z_bf[:, at : at + width, :].rearrange("p v t -> p (v t)"),
+                )
+                prod = psum.tile([P, width], F32, name="prod", tag="prod", bufs=1)
+                nc.tensor.matmul_mx(
+                    out=prod[:],
+                    lhsT=w2_codes[:].bitcast(FP8X4),
+                    lhsT_scale=w2_plane[:],
+                    rhs=z_codes[:].bitcast(FP8X4),
+                    rhs_scale=z_plane[:],
+                    start=True,
+                    stop=True,
+                )
+                result = ring.tile([P, width], F32, name="result", tag="result", bufs=4)
+                if last:
+                    nc.vector.tensor_copy(out=result[:], in_=prod[:])
+                else:
+                    nc.scalar.copy(out=result[:], in_=prod[:])
+                nc.sync.dma_start(out=out[:, v0 + at : v0 + at + width], in_=result[:])
+            v0 = v0 + n

@@ -19,6 +19,8 @@ MULT = mybir.AluOpType.mult
 P = 128
 BANK = 512
 CHUNKS = (512, 384, 128)
+BEHIND = {(0, 1, 0): "w_bf2", (0, 1, 1): "w_bf3", (1, 2, 0): "z_bf0"}
+W_LOADS = ((0, 128), (128, 128), (256, 256))
 
 
 def load_scale_rows(queue, plane, rows):
@@ -46,29 +48,38 @@ def tile_picked_wlapl_gelu_l_kernel(
 
         x_plane = keep.tile([P, T], U8, align_bytes=64)
         w2_plane = keep.tile([P, N], U8, align_bytes=64)
-        nc.vector.memset(x_plane[:].bitcast(I32), 0)
+        nc.gpsimd.memset(x_plane[:].bitcast(I32), 0)
         warm = keep.tile([P, 2], F32)
         nc.vector.memset(warm[:, 0:1], 0.0)
         nc.vector.memset(w2_plane[:].bitcast(I32), 0)
 
         w1_rows = w1.rearrange("(p j) c -> p j c", j=4)
-        w_raw = [keep.tile([P, 4, P], F32, name=f"w_raw{c}") for c in range(4)]
-        x_codes = [keep.tile([P, BANK], U32, name=f"x_codes{s}", align_bytes=64) for s in range(2)]
+        w_tiles = [keep.tile([P, 4, cols], F32, name=f"w_raw{cols0}") for cols0, cols in W_LOADS]
+        w_raw = [w_tiles[0][:], w_tiles[1][:], w_tiles[2][:, :, 0:P], w_tiles[2][:, :, P : 2 * P]]
+        x_all = keep.tile([P, T], U32, align_bytes=64)
+        x_codes = [x_all[:, 0:BANK], x_all[:, BANK:T]]
         x_bytes = x_words[0].rearrange("p n t -> p (n t)")
-        gate_cols = keep.tile([P, 2, 8], F32)
+        gate_cols = [keep.tile([P, 2, 4], F32, name=f"gate_cols{s}") for s in range(2)]
         lists = [keep.tile([P, T // 16], U16, name=f"list{d}") for d in range(2)]
         w2_codes = keep.tile([P, N], U32, align_bytes=64)
 
-        nc.sync.dma_start(out=w_raw[0][:], in_=w1_rows[:, :, 0:P])
-        nc.sync.dma_start(out=x_codes[0][:].bitcast(I32), in_=x_bytes[:, 0 : 4 * BANK].bitcast(I32))
-        load_scale_rows(nc.scalar, x_plane, x_scales[0])
-        nc.sync.dma_start(out=gate_cols[:], in_=gate[:, 0, :].rearrange("d (n j) -> n d j", j=8))
-        nc.sync.dma_start(out=x_codes[1][:].bitcast(I32), in_=x_bytes[:, 4 * BANK : 8 * BANK].bitcast(I32))
-        nc.sync.dma_start(out=w_raw[1][:], in_=w1_rows[:, :, P : 2 * P])
+        def load_gate(s):
+            row = gate[:, 0, s * BANK : (s + 1) * BANK]
+            nc.sync.dma_start(out=gate_cols[s][:], in_=row.rearrange("d (n j) -> n d j", j=4))
+
+        def load_w1(i):
+            cols0, cols = W_LOADS[i]
+            nc.sync.dma_start(out=w_tiles[i][:], in_=w1_rows[:, :, cols0 : cols0 + cols])
+
+        load_w1(0)
+        load_gate(0)
+        load_scale_rows(nc.sync, x_plane, x_scales[0])
+        nc.sync.dma_start(out=x_all[:].bitcast(I32), in_=x_bytes.bitcast(I32))
+        load_w1(1)
         nc.sync.dma_start(lists[0][:], pos1)
         nc.sync.dma_start(lists[1][:], pos2)
-        for c in (2, 3):
-            nc.sync.dma_start(out=w_raw[c][:], in_=w1_rows[:, :, c * P : (c + 1) * P])
+        load_w1(2)
+        load_gate(1)
         nc.sync.dma_start(out=w2_codes[:].bitcast(I32), in_=w2_words[0].rearrange("p n t -> p (n t)").bitcast(I32))
         load_scale_rows(nc.sync, w2_plane, w2_scales[0])
 
@@ -76,94 +87,109 @@ def tile_picked_wlapl_gelu_l_kernel(
         ident = keep.tile([P, P], F32)
         make_identity(nc, ident[:])
 
-        minus_gate = [keep.tile([P, T], F32, name=f"minus_gate{d}") for d in range(2)]
-        for d in range(2):
-            for half in range(2):
-                spread = psum.tile([P, 4, P], F32, name="spread", tag="sum", bufs=5)
+        minus_gate = [[keep.tile([P, BANK], F32, name=f"minus_gate{s}{d}") for d in range(2)] for s in range(2)]
+
+        def spread_gate(s):
+            for d in range(2):
+                if s == 0:
+                    spread = psum.tile([P, 4, P], F32, name="spread", tag="pair", bufs=2)
+                else:
+                    spread = psum.tile([P, 4, P], F32, name="spread", tag="sum", bufs=4)
                 for j in range(4):
-                    col = 4 * half + j
-                    nc.tensor.transpose(spread[:, j, :], gate_cols[:, d, col : col + 1].to_broadcast([P, P]), ident[:])
+                    nc.tensor.transpose(spread[:, j, :], gate_cols[s][:, d, j : j + 1].to_broadcast([P, P]), ident[:])
                 nc.scalar.activation(
-                    out=minus_gate[d][:].rearrange("q (n h j) -> q h n j", h=2, j=4)[:, half],
+                    out=minus_gate[s][d][:].rearrange("q (n j) -> q n j", j=4),
                     in_=spread[:].rearrange("q j n -> q n j"),
                     func=ACT.Copy,
                     scale=-1.0,
                 )
 
-        w_codes, w_planes = [], []
-        w_bf = []
-        for c in range(4):
-            bf = keep.tile([P, P, 4], BF16, name=f"w_bf{c}", align_bytes=64)
-            nc.vector.tensor_copy(
+        spread_gate(0)
+
+        def quantise_w1(c, copy):
+            bf = ring.tile([P, P, 4], BF16, name=f"w_bf{c}", tag=f"w_bf{c}", align_bytes=64)
+            copy(
                 out=bf[:].rearrange("p (m i) j -> p m j i", i=4),
-                in_=w_raw[c][:].rearrange("p j (m i) -> p m j i", i=4),
+                in_=w_raw[c].rearrange("p j (m i) -> p m j i", i=4),
             )
             codes = keep.tile([P, P], U32, name=f"w_codes{c}", align_bytes=64)
             plane = keep.tile([P, P], U8, name=f"w_plane{c}", align_bytes=64)
             nc.vector.quantize_mx(
                 out=codes[:].bitcast(FP8X4), scales=plane[:], in_=bf[:].rearrange("p m j -> p (m j)")
             )
-            w_codes.append(codes)
-            w_planes.append(plane)
+            return codes, plane
 
         h = [keep.tile([P, T], F32, name=f"h{c}") for c in range(4)]
-        for c in range(4):
+
+        def first_product(c, codes, plane):
             for s in range(2):
                 cols = slice(s * BANK, (s + 1) * BANK)
                 pre = psum.tile([P, BANK], F32, name="pre", tag="pair", bufs=2)
                 nc.tensor.matmul_mx(
                     out=pre[:],
-                    lhsT=w_codes[c][:].bitcast(FP8X4),
-                    lhsT_scale=w_planes[c][:],
-                    rhs=x_codes[s][:].bitcast(FP8X4),
+                    lhsT=codes[:].bitcast(FP8X4),
+                    lhsT_scale=plane[:],
+                    rhs=x_codes[s].bitcast(FP8X4),
                     rhs_scale=x_plane[:, cols],
                     start=True,
                     stop=True,
                 )
                 nc.scalar.activation(out=h[c][:, cols], in_=pre[:], func=ACT.Gelu_apprx_tanh)
 
+        w_mx = [quantise_w1(c, nc.vector.tensor_copy) for c in range(2)]
+        for c in range(4):
+            first_product(c, *w_mx[c])
+            if c < 2:
+                w_mx.append(quantise_w1(c + 2, nc.scalar.copy))
+
         v0 = 0
         for ci, n in enumerate(CHUNKS):
             last = ci == len(CHUNKS) - 1
             blocks = n // P
-            sums = [psum.tile([P, H], F32, name="sums", tag="sum", bufs=5) for b in range(blocks)]
+            if ci == 1:
+                spread_gate(1)
+            z_rows = ring.tile([P, blocks, 2, P, 2], BF16, name=f"z_rows{ci}")
             for c in range(4):
                 terms = []
                 for d in range(2):
-                    term = ring.tile([P, n], F32, name="term", tag="term", bufs=8)
+                    if (ci, c, d) in BEHIND:
+                        term = ring.tile([P, n], F32, name="term_late", tag=BEHIND[(ci, c, d)], align_bytes=64)
+                    else:
+                        term = ring.tile([P, n], F32, name="term", tag="term", bufs=6)
                     nc.vector.tensor_tensor(
                         term[:],
                         h[c][:].indirect(lists[d][:, v0 // 16 : (v0 + n) // 16]),
-                        minus_gate[d][:, v0 : v0 + n],
+                        minus_gate[v0 // BANK][d][:, v0 % BANK : v0 % BANK + n],
                         MULT,
                     )
                     terms.append(term)
-                for b in range(blocks):
-                    parts = [h[c][:, v0 + b * P : v0 + (b + 1) * P]] + [t[:, b * P : (b + 1) * P] for t in terms]
-                    for i, part in enumerate(parts):
+                sums = psum.tile([P, blocks, P], F32, name="sums", tag="sum", bufs=4)
+                parts = [h[c][:, v0 : v0 + n]] + [t[:] for t in terms]
+                for i, part in enumerate(parts):
+                    for b in range(blocks):
                         nc.tensor.matmul(
-                            sums[b][:, c * P : (c + 1) * P],
-                            lhsT=part,
+                            sums[:, b, :],
+                            lhsT=part[:, b * P : (b + 1) * P],
                             rhs=ident[:],
-                            start=(i == 0),
-                            stop=(i == 2),
+                            start=(i == 0 and b == 0),
+                            stop=(i == 2 and b == blocks - 1),
                             is_transpose=True,
                         )
+                nc.scalar.copy(
+                    out=z_rows[:, :, :, 32 * c : 32 * (c + 1), :],
+                    in_=sums[:].rearrange("v b (p u e) -> v b u p e", u=2, e=2),
+                )
 
-            z_bf = ring.tile([P, n, 4], BF16, name="z_bf", tag="z_bf", bufs=3, align_bytes=64)
+            z_bf = ring.tile([P, n, 4], BF16, name=f"z_bf{ci}", tag=f"z_bf{ci}", align_bytes=64)
             z_words = z_bf[:].rearrange("p v t -> p (v t)").bitcast(F32)
+            pairs = z_rows[:].rearrange("v b u p e -> v (b u p e)").bitcast(F32)
             for b0 in range(0, blocks, 2):
                 nb = min(2, blocks - b0)
                 back = psum.tile([P, nb, 2, P], F32, name="back", tag="pair", bufs=2)
                 for b in range(b0, b0 + nb):
-                    z_rows = ring.tile([P, H], BF16, name="z_rows", tag="z_rows", bufs=3)
-                    nc.scalar.copy(
-                        out=z_rows[:].rearrange("v (u p e) -> v u p e", u=2, e=2),
-                        in_=sums[b][:].rearrange("v (p u e) -> v u p e", u=2, e=2),
-                    )
-                    pairs = z_rows[:].bitcast(F32)
                     for u in range(2):
-                        nc.tensor.transpose(back[:, b - b0, u, :], pairs[:, u * P : (u + 1) * P], ident[:])
+                        at = (2 * b + u) * P
+                        nc.tensor.transpose(back[:, b - b0, u, :], pairs[:, at : at + P], ident[:])
                 nc.scalar.copy(
                     out=z_words[:, 2 * P * b0 : 2 * P * (b0 + nb)].rearrange("p (b v u) -> p b v u", b=nb, u=2),
                     in_=back[:].rearrange("p b u v -> p b v u"),
@@ -177,7 +203,7 @@ def tile_picked_wlapl_gelu_l_kernel(
                     scales=z_plane[:],
                     in_=z_bf[:, at : at + width, :].rearrange("p v t -> p (v t)"),
                 )
-                prod = psum.tile([P, width], F32, name="prod", tag="prod", bufs=1)
+                prod = psum.tile([P, width], F32, name="prod", tag="prod", bufs=2)
                 nc.tensor.matmul_mx(
                     out=prod[:],
                     lhsT=w2_codes[:].bitcast(FP8X4),
@@ -188,9 +214,9 @@ def tile_picked_wlapl_gelu_l_kernel(
                     stop=True,
                 )
                 result = ring.tile([P, width], F32, name="result", tag="result", bufs=4)
-                if last:
+                if ci == 1:
                     nc.vector.tensor_copy(out=result[:], in_=prod[:])
                 else:
                     nc.scalar.copy(out=result[:], in_=prod[:])
-                nc.sync.dma_start(out=out[:, v0 + at : v0 + at + width], in_=result[:])
+                (nc.scalar if last else nc.sync).dma_start(out=out[:, v0 + at : v0 + at + width], in_=result[:])
             v0 = v0 + n

@@ -15,11 +15,13 @@ U8 = mybir.dt.uint8
 FP8X4 = mybir.dt.float8_e4m3fn_x4
 ACT = mybir.ActivationFunctionType
 MULT = mybir.AluOpType.mult
+ADD = mybir.AluOpType.add
 
 P = 128
 BANK = 512
 CHUNKS = (512, 384, 128)
-BEHIND = {(0, 1, 0): "w_bf2", (0, 1, 1): "w_bf3", (1, 2, 0): "z_bf0"}
+BEHIND = {(0, 1, 0): "w_codes0", (0, 1, 1): "w_codes1", (1, 1, 0): "z_bf0"}
+VECTOR_ADDS = ((0, 1), (0, 2), (0, 3))
 W_LOADS = ((0, 128), (128, 128), (256, 256))
 
 
@@ -56,30 +58,28 @@ def tile_picked_wlapl_gelu_l_kernel(
         w1_rows = w1.rearrange("(p j) c -> p j c", j=4)
         w_tiles = [keep.tile([P, 4, cols], F32, name=f"w_raw{cols0}") for cols0, cols in W_LOADS]
         w_raw = [w_tiles[0][:], w_tiles[1][:], w_tiles[2][:, :, 0:P], w_tiles[2][:, :, P : 2 * P]]
-        x_all = keep.tile([P, T], U32, align_bytes=64)
-        x_codes = [x_all[:, 0:BANK], x_all[:, BANK:T]]
+        x_codes = [keep.tile([P, BANK], U32, name=f"x_codes{s}", align_bytes=64) for s in range(2)]
         x_bytes = x_words[0].rearrange("p n t -> p (n t)")
-        gate_cols = [keep.tile([P, 2, 4], F32, name=f"gate_cols{s}") for s in range(2)]
+        gate_cols = keep.tile([P, 2, 4], F32)
+        gate_late = [keep.tile([P, BANK], F32, name=f"gate_late{d}") for d in range(2)]
         lists = [keep.tile([P, T // 16], U16, name=f"list{d}") for d in range(2)]
         w2_codes = keep.tile([P, N], U32, align_bytes=64)
-
-        def load_gate(s):
-            row = gate[:, 0, s * BANK : (s + 1) * BANK]
-            nc.sync.dma_start(out=gate_cols[s][:], in_=row.rearrange("d (n j) -> n d j", j=4))
 
         def load_w1(i):
             cols0, cols = W_LOADS[i]
             nc.sync.dma_start(out=w_tiles[i][:], in_=w1_rows[:, :, cols0 : cols0 + cols])
 
+        nc.sync.dma_start(out=gate_cols[:], in_=gate[:, 0, 0:BANK].rearrange("d (n j) -> n d j", j=4))
         load_w1(0)
-        load_gate(0)
         load_scale_rows(nc.sync, x_plane, x_scales[0])
-        nc.sync.dma_start(out=x_all[:].bitcast(I32), in_=x_bytes.bitcast(I32))
+        for s in range(2):
+            nc.sync.dma_start(out=x_codes[s][:].bitcast(I32), in_=x_bytes[:, 4 * BANK * s : 4 * BANK * (s + 1)].bitcast(I32))
         load_w1(1)
         nc.sync.dma_start(lists[0][:], pos1)
         nc.sync.dma_start(lists[1][:], pos2)
         load_w1(2)
-        load_gate(1)
+        for d in range(2):
+            nc.sync.dma_start(out=gate_late[d][:], in_=gate[d, :, BANK:T])
         nc.sync.dma_start(out=w2_codes[:].bitcast(I32), in_=w2_words[0].rearrange("p n t -> p (n t)").bitcast(I32))
         load_scale_rows(nc.sync, w2_plane, w2_scales[0])
 
@@ -87,32 +87,26 @@ def tile_picked_wlapl_gelu_l_kernel(
         ident = keep.tile([P, P], F32)
         make_identity(nc, ident[:])
 
-        minus_gate = [[keep.tile([P, BANK], F32, name=f"minus_gate{s}{d}") for d in range(2)] for s in range(2)]
+        minus_gate = [[keep.tile([P, BANK], F32, name=f"minus_gate0{d}") for d in range(2)], []]
 
-        def spread_gate(s):
-            for d in range(2):
-                if s == 0:
-                    spread = psum.tile([P, 4, P], F32, name="spread", tag="pair", bufs=2)
-                else:
-                    spread = psum.tile([P, 4, P], F32, name="spread", tag="sum", bufs=4)
-                for j in range(4):
-                    nc.tensor.transpose(spread[:, j, :], gate_cols[s][:, d, j : j + 1].to_broadcast([P, P]), ident[:])
-                nc.scalar.activation(
-                    out=minus_gate[s][d][:].rearrange("q (n j) -> q n j", j=4),
-                    in_=spread[:].rearrange("q j n -> q n j"),
-                    func=ACT.Copy,
-                    scale=-1.0,
-                )
-
-        spread_gate(0)
+        for d in range(2):
+            spread = psum.tile([P, 4, P], F32, name="spread", tag="pair", bufs=2)
+            for j in range(4):
+                nc.tensor.transpose(spread[:, j, :], gate_cols[:, d, j : j + 1].to_broadcast([P, P]), ident[:])
+            nc.scalar.activation(
+                out=minus_gate[0][d][:].rearrange("q (n j) -> q n j", j=4),
+                in_=spread[:].rearrange("q j n -> q n j"),
+                func=ACT.Copy,
+                scale=-1.0,
+            )
 
         def quantise_w1(c, copy):
-            bf = ring.tile([P, P, 4], BF16, name=f"w_bf{c}", tag=f"w_bf{c}", align_bytes=64)
+            bf = ring.tile([P, P, 4], BF16, name=f"w_bf{c}", tag=f"w_bf{c}" if c < 2 else f"w_codes{c - 2}", align_bytes=64)
             copy(
                 out=bf[:].rearrange("p (m i) j -> p m j i", i=4),
                 in_=w_raw[c].rearrange("p j (m i) -> p m j i", i=4),
             )
-            codes = keep.tile([P, P], U32, name=f"w_codes{c}", align_bytes=64)
+            codes = ring.tile([P, P], U32, name=f"w_codes{c}", tag=f"w_codes{c}", align_bytes=64)
             plane = keep.tile([P, P], U8, name=f"w_plane{c}", align_bytes=64)
             nc.vector.quantize_mx(
                 out=codes[:].bitcast(FP8X4), scales=plane[:], in_=bf[:].rearrange("p m j -> p (m j)")
@@ -129,7 +123,7 @@ def tile_picked_wlapl_gelu_l_kernel(
                     out=pre[:],
                     lhsT=codes[:].bitcast(FP8X4),
                     lhsT_scale=plane[:],
-                    rhs=x_codes[s].bitcast(FP8X4),
+                    rhs=x_codes[s][:].bitcast(FP8X4),
                     rhs_scale=x_plane[:, cols],
                     start=True,
                     stop=True,
@@ -147,7 +141,10 @@ def tile_picked_wlapl_gelu_l_kernel(
             last = ci == len(CHUNKS) - 1
             blocks = n // P
             if ci == 1:
-                spread_gate(1)
+                for d in range(2):
+                    late = ring.tile([P, BANK], F32, name=f"minus_gate1{d}", tag=f"w_codes{2 + d}", align_bytes=64)
+                    minus_gate[1].append(late)
+                    nc.scalar.activation(out=minus_gate[1][d][:], in_=gate_late[d][:], func=ACT.Copy, scale=-1.0)
             z_rows = ring.tile([P, blocks, 2, P, 2], BF16, name=f"z_rows{ci}")
             for c in range(4):
                 terms = []
@@ -155,7 +152,7 @@ def tile_picked_wlapl_gelu_l_kernel(
                     if (ci, c, d) in BEHIND:
                         term = ring.tile([P, n], F32, name="term_late", tag=BEHIND[(ci, c, d)], align_bytes=64)
                     else:
-                        term = ring.tile([P, n], F32, name="term", tag="term", bufs=6)
+                        term = ring.tile([P, n], F32, name="term", tag="term", bufs=4)
                     nc.vector.tensor_tensor(
                         term[:],
                         h[c][:].indirect(lists[d][:, v0 // 16 : (v0 + n) // 16]),
@@ -165,6 +162,10 @@ def tile_picked_wlapl_gelu_l_kernel(
                     terms.append(term)
                 sums = psum.tile([P, blocks, P], F32, name="sums", tag="sum", bufs=4)
                 parts = [h[c][:, v0 : v0 + n]] + [t[:] for t in terms]
+                if (ci, c) in VECTOR_ADDS:
+                    joined = ring.tile([P, n], F32, name="joined", tag="joined", bufs=3)
+                    nc.vector.tensor_tensor(joined[:], parts[0], parts[1], ADD)
+                    parts = [parts[2], joined[:]]
                 for i, part in enumerate(parts):
                     for b in range(blocks):
                         nc.tensor.matmul(
@@ -172,7 +173,7 @@ def tile_picked_wlapl_gelu_l_kernel(
                             lhsT=part[:, b * P : (b + 1) * P],
                             rhs=ident[:],
                             start=(i == 0 and b == 0),
-                            stop=(i == 2 and b == blocks - 1),
+                            stop=(i == len(parts) - 1 and b == blocks - 1),
                             is_transpose=True,
                         )
                 nc.scalar.copy(

@@ -21,7 +21,7 @@ P = 128
 BANK = 512
 CHUNKS = (512, 384, 128)
 BEHIND = {(0, 1, 0): "w_codes0", (0, 1, 1): "w_codes1", (1, 1, 0): "z_bf0"}
-VECTOR_ADDS = ((0, 1), (0, 2), (0, 3))
+VECTOR_ADDS = ()
 W_LOADS = ((0, 128), (128, 128), (256, 256))
 
 
@@ -69,8 +69,8 @@ def tile_picked_wlapl_gelu_l_kernel(
             cols0, cols = W_LOADS[i]
             nc.sync.dma_start(out=w_tiles[i][:], in_=w1_rows[:, :, cols0 : cols0 + cols])
 
-        nc.sync.dma_start(out=gate_cols[:], in_=gate[:, 0, 0:BANK].rearrange("d (n j) -> n d j", j=4))
         load_w1(0)
+        nc.sync.dma_start(out=gate_cols[:], in_=gate[:, 0, 0:BANK].rearrange("d (n j) -> n d j", j=4))
         load_scale_rows(nc.sync, x_plane, x_scales[0])
         for s in range(2):
             nc.sync.dma_start(out=x_codes[s][:].bitcast(I32), in_=x_bytes[:, 4 * BANK * s : 4 * BANK * (s + 1)].bitcast(I32))
@@ -89,7 +89,7 @@ def tile_picked_wlapl_gelu_l_kernel(
 
         minus_gate = [[keep.tile([P, BANK], F32, name=f"minus_gate0{d}") for d in range(2)], []]
 
-        for d in range(2):
+        def spread_gate(d):
             spread = psum.tile([P, 4, P], F32, name="spread", tag="pair", bufs=2)
             for j in range(4):
                 nc.tensor.transpose(spread[:, j, :], gate_cols[:, d, j : j + 1].to_broadcast([P, P]), ident[:])
@@ -99,6 +99,8 @@ def tile_picked_wlapl_gelu_l_kernel(
                 func=ACT.Copy,
                 scale=-1.0,
             )
+
+        spread_gate(0)
 
         def quantise_w1(c, copy):
             bf = ring.tile([P, P, 4], BF16, name=f"w_bf{c}", tag=f"w_bf{c}" if c < 2 else f"w_codes{c - 2}", align_bytes=64)
@@ -133,8 +135,37 @@ def tile_picked_wlapl_gelu_l_kernel(
         w_mx = [quantise_w1(c, nc.vector.tensor_copy) for c in range(2)]
         for c in range(4):
             first_product(c, *w_mx[c])
+            if c == 0:
+                spread_gate(1)
             if c < 2:
                 w_mx.append(quantise_w1(c + 2, nc.scalar.copy))
+
+        def second_product(ci, v0, n, z_bf):
+            last = ci == len(CHUNKS) - 1
+            for at, width in mx_pieces(n):
+                z_codes = ring.tile([P, width], U32, name="z_codes", tag="z_codes", bufs=4, align_bytes=64)
+                z_plane = ring.tile([P, width], U8, name="z_plane", tag="z_plane", bufs=4, align_bytes=64)
+                nc.vector.quantize_mx(
+                    out=z_codes[:].bitcast(FP8X4),
+                    scales=z_plane[:],
+                    in_=z_bf[:, at : at + width, :].rearrange("p v t -> p (v t)"),
+                )
+                prod = psum.tile([P, width], F32, name="prod", tag="prod", bufs=2)
+                nc.tensor.matmul_mx(
+                    out=prod[:],
+                    lhsT=w2_codes[:].bitcast(FP8X4),
+                    lhsT_scale=w2_plane[:],
+                    rhs=z_codes[:].bitcast(FP8X4),
+                    rhs_scale=z_plane[:],
+                    start=True,
+                    stop=True,
+                )
+                result = ring.tile([P, width], F32, name="result", tag="result", bufs=4)
+                if ci == 1:
+                    nc.vector.tensor_copy(out=result[:], in_=prod[:])
+                else:
+                    nc.scalar.copy(out=result[:], in_=prod[:])
+                (nc.scalar if last else nc.sync).dma_start(out=out[:, v0 + at : v0 + at + width], in_=result[:])
 
         v0 = 0
         for ci, n in enumerate(CHUNKS):
@@ -196,28 +227,10 @@ def tile_picked_wlapl_gelu_l_kernel(
                     in_=back[:].rearrange("p b u v -> p b v u"),
                 )
 
-            for at, width in mx_pieces(n):
-                z_codes = ring.tile([P, width], U32, name="z_codes", tag="z_codes", bufs=4, align_bytes=64)
-                z_plane = ring.tile([P, width], U8, name="z_plane", tag="z_plane", bufs=4, align_bytes=64)
-                nc.vector.quantize_mx(
-                    out=z_codes[:].bitcast(FP8X4),
-                    scales=z_plane[:],
-                    in_=z_bf[:, at : at + width, :].rearrange("p v t -> p (v t)"),
-                )
-                prod = psum.tile([P, width], F32, name="prod", tag="prod", bufs=2)
-                nc.tensor.matmul_mx(
-                    out=prod[:],
-                    lhsT=w2_codes[:].bitcast(FP8X4),
-                    lhsT_scale=w2_plane[:],
-                    rhs=z_codes[:].bitcast(FP8X4),
-                    rhs_scale=z_plane[:],
-                    start=True,
-                    stop=True,
-                )
-                result = ring.tile([P, width], F32, name="result", tag="result", bufs=4)
-                if ci == 1:
-                    nc.vector.tensor_copy(out=result[:], in_=prod[:])
-                else:
-                    nc.scalar.copy(out=result[:], in_=prod[:])
-                (nc.scalar if last else nc.sync).dma_start(out=out[:, v0 + at : v0 + at + width], in_=result[:])
+            if ci == 1:
+                waiting = (ci, v0, n, z_bf)
+            else:
+                if last:
+                    second_product(*waiting)
+                second_product(ci, v0, n, z_bf)
             v0 = v0 + n

@@ -18,16 +18,23 @@ MULT = mybir.AluOpType.mult
 ADD = mybir.AluOpType.add
 
 P = 128
+PACK = 4
 BANK = 512
+LANES = 16
+TILES = H // P
+LISTS = 2
+
 CHUNKS = (512, 384, 128)
-BEHIND = {(0, 1, 0): "w_codes0", (0, 1, 1): "w_codes1", (1, 1, 0): "z_bf0"}
-VECTOR_ADDS = ()
-W_LOADS = ((0, 128), (128, 128), (256, 256))
+W1_LOADS = ((0, 128), (128, 128), (256, 256))
+VECTOR_ADD = (0, 2)
+BEHIND_QUANTISE = {(0, 1, 0): "w1_codes0", (0, 1, 1): "w1_codes1", (1, 1, 0): "z_packed0"}
+TERM_BUFS = 4
+SHORT_BANKS, SUM_BANKS, OUT_BANKS = 3, 3, 2
 
 
-def load_scale_rows(queue, plane, rows):
+def load_scale_rows(nc, plane, rows):
     for q in range(4):
-        queue.dma_start(out=plane[32 * q : 32 * q + 4, :].bitcast(I32), in_=rows[4 * q : 4 * q + 4, :].bitcast(I32))
+        nc.sync.dma_start(out=plane[32 * q : 32 * q + 4, :].bitcast(I32), in_=rows[4 * q : 4 * q + 4, :].bitcast(I32))
 
 
 def mx_pieces(n):
@@ -55,42 +62,43 @@ def tile_picked_wlapl_gelu_l_kernel(
         nc.vector.memset(warm[:, 0:1], 0.0)
         nc.vector.memset(w2_plane[:].bitcast(I32), 0)
 
-        w1_rows = w1.rearrange("(p j) c -> p j c", j=4)
-        w_tiles = [keep.tile([P, 4, cols], F32, name=f"w_raw{cols0}") for cols0, cols in W_LOADS]
-        w_raw = [w_tiles[0][:], w_tiles[1][:], w_tiles[2][:, :, 0:P], w_tiles[2][:, :, P : 2 * P]]
-        x_codes = [keep.tile([P, BANK], U32, name=f"x_codes{s}", align_bytes=64) for s in range(2)]
+        w1_rows = w1.rearrange("(p j) c -> p j c", j=PACK)
+        w1_loaded = [keep.tile([P, PACK, cols], F32, name=f"w1_loaded{first}") for first, cols in W1_LOADS]
+        w1_raw = [w1_loaded[0][:], w1_loaded[1][:], w1_loaded[2][:, :, 0:P], w1_loaded[2][:, :, P : 2 * P]]
+        x_codes = [keep.tile([P, BANK], U32, name=f"x_codes{half}", align_bytes=64) for half in range(2)]
         x_bytes = x_words[0].rearrange("p n t -> p (n t)")
-        gate_cols = keep.tile([P, 2, 4], F32)
-        gate_late = [keep.tile([P, BANK], F32, name=f"gate_late{d}") for d in range(2)]
-        lists = [keep.tile([P, T // 16], U16, name=f"list{d}") for d in range(2)]
+        gate_cols = keep.tile([P, LISTS, 4], F32)
+        gate_late = [keep.tile([P, BANK], F32, name=f"gate_late{d}") for d in range(LISTS)]
+        lists = [keep.tile([P, T // LANES], U16, name=f"list{d}") for d in range(LISTS)]
         w2_codes = keep.tile([P, N], U32, align_bytes=64)
 
         def load_w1(i):
-            cols0, cols = W_LOADS[i]
-            nc.sync.dma_start(out=w_tiles[i][:], in_=w1_rows[:, :, cols0 : cols0 + cols])
+            first, cols = W1_LOADS[i]
+            nc.sync.dma_start(out=w1_loaded[i][:], in_=w1_rows[:, :, first : first + cols])
 
         load_w1(0)
         nc.sync.dma_start(out=gate_cols[:], in_=gate[:, 0, 0:BANK].rearrange("d (n j) -> n d j", j=4))
-        load_scale_rows(nc.sync, x_plane, x_scales[0])
-        for s in range(2):
-            nc.sync.dma_start(out=x_codes[s][:].bitcast(I32), in_=x_bytes[:, 4 * BANK * s : 4 * BANK * (s + 1)].bitcast(I32))
+        load_scale_rows(nc, x_plane, x_scales[0])
+        for half in range(2):
+            half_bytes = x_bytes[:, PACK * BANK * half : PACK * BANK * (half + 1)]
+            nc.sync.dma_start(out=x_codes[half][:].bitcast(I32), in_=half_bytes.bitcast(I32))
         load_w1(1)
         nc.sync.dma_start(lists[0][:], pos1)
         nc.sync.dma_start(lists[1][:], pos2)
         load_w1(2)
-        for d in range(2):
+        for d in range(LISTS):
             nc.sync.dma_start(out=gate_late[d][:], in_=gate[d, :, BANK:T])
         nc.sync.dma_start(out=w2_codes[:].bitcast(I32), in_=w2_words[0].rearrange("p n t -> p (n t)").bitcast(I32))
-        load_scale_rows(nc.sync, w2_plane, w2_scales[0])
+        load_scale_rows(nc, w2_plane, w2_scales[0])
 
         nc.scalar.activation(out=warm[:, 1:2], in_=warm[:, 0:1], func=ACT.Gelu_apprx_tanh)
         ident = keep.tile([P, P], F32)
         make_identity(nc, ident[:])
 
-        minus_gate = [[keep.tile([P, BANK], F32, name=f"minus_gate0{d}") for d in range(2)], []]
+        minus_gate = [[keep.tile([P, BANK], F32, name=f"minus_gate0{d}") for d in range(LISTS)], []]
 
         def spread_gate(d):
-            spread = psum.tile([P, 4, P], F32, name="spread", tag="pair", bufs=2)
+            spread = psum.tile([P, 4, P], F32, name="spread", tag="short", bufs=SHORT_BANKS)
             for j in range(4):
                 nc.tensor.transpose(spread[:, j, :], gate_cols[:, d, j : j + 1].to_broadcast([P, P]), ident[:])
             nc.scalar.activation(
@@ -103,98 +111,66 @@ def tile_picked_wlapl_gelu_l_kernel(
         spread_gate(0)
 
         def quantise_w1(c, copy):
-            bf = ring.tile([P, P, 4], BF16, name=f"w_bf{c}", tag=f"w_bf{c}" if c < 2 else f"w_codes{c - 2}", align_bytes=64)
+            tag = f"w1_packed{c}" if c < 2 else f"w1_codes{c - 2}"
+            packed = ring.tile([P, P, PACK], BF16, name=f"w1_packed{c}", tag=tag, align_bytes=64)
             copy(
-                out=bf[:].rearrange("p (m i) j -> p m j i", i=4),
-                in_=w_raw[c].rearrange("p j (m i) -> p m j i", i=4),
+                out=packed[:].rearrange("p (m i) j -> p m j i", i=4),
+                in_=w1_raw[c].rearrange("p j (m i) -> p m j i", i=4),
             )
-            codes = ring.tile([P, P], U32, name=f"w_codes{c}", tag=f"w_codes{c}", align_bytes=64)
-            plane = keep.tile([P, P], U8, name=f"w_plane{c}", align_bytes=64)
+            codes = ring.tile([P, P], U32, name=f"w1_codes{c}", tag=f"w1_codes{c}", align_bytes=64)
+            plane = keep.tile([P, P], U8, name=f"w1_plane{c}", align_bytes=64)
             nc.vector.quantize_mx(
-                out=codes[:].bitcast(FP8X4), scales=plane[:], in_=bf[:].rearrange("p m j -> p (m j)")
+                out=codes[:].bitcast(FP8X4), scales=plane[:], in_=packed[:].rearrange("p m j -> p (m j)")
             )
             return codes, plane
 
-        h = [keep.tile([P, T], F32, name=f"h{c}") for c in range(4)]
+        h = [keep.tile([P, T], F32, name=f"h{c}") for c in range(TILES)]
 
         def first_product(c, codes, plane):
-            for s in range(2):
-                cols = slice(s * BANK, (s + 1) * BANK)
-                pre = psum.tile([P, BANK], F32, name="pre", tag="pair", bufs=2)
+            width = BANK // 2 if c == 0 else BANK
+            for at in range(0, T, width):
+                cols = slice(at, at + width)
+                pre = psum.tile([P, width], F32, name="pre", tag="short", bufs=SHORT_BANKS)
                 nc.tensor.matmul_mx(
                     out=pre[:],
                     lhsT=codes[:].bitcast(FP8X4),
                     lhsT_scale=plane[:],
-                    rhs=x_codes[s][:].bitcast(FP8X4),
+                    rhs=x_codes[at // BANK][:, at % BANK : at % BANK + width].bitcast(FP8X4),
                     rhs_scale=x_plane[:, cols],
                     start=True,
                     stop=True,
                 )
                 nc.scalar.activation(out=h[c][:, cols], in_=pre[:], func=ACT.Gelu_apprx_tanh)
 
-        w_mx = [quantise_w1(c, nc.vector.tensor_copy) for c in range(2)]
-        for c in range(4):
-            first_product(c, *w_mx[c])
+        w1_mx = [quantise_w1(c, nc.vector.tensor_copy) for c in range(2)]
+        for c in range(TILES):
+            first_product(c, *w1_mx[c])
             if c == 0:
                 spread_gate(1)
             if c < 2:
-                w_mx.append(quantise_w1(c + 2, nc.scalar.copy))
+                w1_mx.append(quantise_w1(c + 2, nc.scalar.copy))
 
-        def second_product(ci, v0, n, z_bf):
-            last = ci == len(CHUNKS) - 1
-            for at, width in mx_pieces(n):
-                z_codes = ring.tile([P, width], U32, name="z_codes", tag="z_codes", bufs=4, align_bytes=64)
-                z_plane = ring.tile([P, width], U8, name="z_plane", tag="z_plane", bufs=4, align_bytes=64)
-                nc.vector.quantize_mx(
-                    out=z_codes[:].bitcast(FP8X4),
-                    scales=z_plane[:],
-                    in_=z_bf[:, at : at + width, :].rearrange("p v t -> p (v t)"),
-                )
-                prod = psum.tile([P, width], F32, name="prod", tag="prod", bufs=2)
-                nc.tensor.matmul_mx(
-                    out=prod[:],
-                    lhsT=w2_codes[:].bitcast(FP8X4),
-                    lhsT_scale=w2_plane[:],
-                    rhs=z_codes[:].bitcast(FP8X4),
-                    rhs_scale=z_plane[:],
-                    start=True,
-                    stop=True,
-                )
-                result = ring.tile([P, width], F32, name="result", tag="result", bufs=4)
-                if ci == 1:
-                    nc.vector.tensor_copy(out=result[:], in_=prod[:])
-                else:
-                    nc.scalar.copy(out=result[:], in_=prod[:])
-                (nc.scalar if last else nc.sync).dma_start(out=out[:, v0 + at : v0 + at + width], in_=result[:])
-
-        v0 = 0
-        for ci, n in enumerate(CHUNKS):
-            last = ci == len(CHUNKS) - 1
+        def sum_chunk(chunk, v0, n):
             blocks = n // P
-            if ci == 1:
-                for d in range(2):
-                    late = ring.tile([P, BANK], F32, name=f"minus_gate1{d}", tag=f"w_codes{2 + d}", align_bytes=64)
-                    minus_gate[1].append(late)
-                    nc.scalar.activation(out=minus_gate[1][d][:], in_=gate_late[d][:], func=ACT.Copy, scale=-1.0)
-            z_rows = ring.tile([P, blocks, 2, P, 2], BF16, name=f"z_rows{ci}")
-            for c in range(4):
+            z_rows = ring.tile([P, blocks, 2, P, 2], BF16, name=f"z_rows{chunk}")
+            for c in range(TILES):
                 terms = []
-                for d in range(2):
-                    if (ci, c, d) in BEHIND:
-                        term = ring.tile([P, n], F32, name="term_late", tag=BEHIND[(ci, c, d)], align_bytes=64)
+                for d in range(LISTS):
+                    if (chunk, c, d) in BEHIND_QUANTISE:
+                        term = ring.tile([P, n], F32, name="term_held", tag=BEHIND_QUANTISE[(chunk, c, d)], align_bytes=64)
                     else:
-                        term = ring.tile([P, n], F32, name="term", tag="term", bufs=4)
+                        term = ring.tile([P, n], F32, name="term", tag="term", bufs=TERM_BUFS)
                     nc.vector.tensor_tensor(
                         term[:],
-                        h[c][:].indirect(lists[d][:, v0 // 16 : (v0 + n) // 16]),
+                        h[c][:].indirect(lists[d][:, v0 // LANES : (v0 + n) // LANES]),
                         minus_gate[v0 // BANK][d][:, v0 % BANK : v0 % BANK + n],
                         MULT,
                     )
                     terms.append(term)
-                sums = psum.tile([P, blocks, P], F32, name="sums", tag="sum", bufs=4)
-                parts = [h[c][:, v0 : v0 + n]] + [t[:] for t in terms]
-                if (ci, c) in VECTOR_ADDS:
-                    joined = ring.tile([P, n], F32, name="joined", tag="joined", bufs=3)
+                sums = psum.tile([P, blocks, P], F32, name="sums", tag="sum", bufs=SUM_BANKS)
+                parts = [h[c][:, v0 : v0 + n]] + [term[:] for term in terms]
+                if (chunk, c) == VECTOR_ADD:
+                    joined = ring.tile([P, n], F32, name="joined")
                     nc.vector.tensor_tensor(joined[:], parts[0], parts[1], ADD)
                     parts = [parts[2], joined[:]]
                 for i, part in enumerate(parts):
@@ -212,12 +188,12 @@ def tile_picked_wlapl_gelu_l_kernel(
                     in_=sums[:].rearrange("v b (p u e) -> v b u p e", u=2, e=2),
                 )
 
-            z_bf = ring.tile([P, n, 4], BF16, name=f"z_bf{ci}", tag=f"z_bf{ci}", align_bytes=64)
-            z_words = z_bf[:].rearrange("p v t -> p (v t)").bitcast(F32)
+            z_packed = ring.tile([P, n, PACK], BF16, name=f"z_packed{chunk}", tag=f"z_packed{chunk}", align_bytes=64)
+            z_words = z_packed[:].rearrange("p v t -> p (v t)").bitcast(F32)
             pairs = z_rows[:].rearrange("v b u p e -> v (b u p e)").bitcast(F32)
             for b0 in range(0, blocks, 2):
                 nb = min(2, blocks - b0)
-                back = psum.tile([P, nb, 2, P], F32, name="back", tag="pair", bufs=2)
+                back = psum.tile([P, nb, 2, P], F32, name="back", tag="short", bufs=SHORT_BANKS)
                 for b in range(b0, b0 + nb):
                     for u in range(2):
                         at = (2 * b + u) * P
@@ -226,11 +202,41 @@ def tile_picked_wlapl_gelu_l_kernel(
                     out=z_words[:, 2 * P * b0 : 2 * P * (b0 + nb)].rearrange("p (b v u) -> p b v u", b=nb, u=2),
                     in_=back[:].rearrange("p b u v -> p b v u"),
                 )
+            return z_packed
 
-            if ci == 1:
-                waiting = (ci, v0, n, z_bf)
-            else:
-                if last:
-                    second_product(*waiting)
-                second_product(ci, v0, n, z_bf)
-            v0 = v0 + n
+        def second_product(v0, n, z_packed, copy, queue):
+            for at, width in mx_pieces(n):
+                z_codes = ring.tile([P, width], U32, name="z_codes", tag="z_codes", bufs=4, align_bytes=64)
+                z_plane = ring.tile([P, width], U8, name="z_plane", tag="z_plane", bufs=4, align_bytes=64)
+                nc.vector.quantize_mx(
+                    out=z_codes[:].bitcast(FP8X4),
+                    scales=z_plane[:],
+                    in_=z_packed[:, at : at + width, :].rearrange("p v t -> p (v t)"),
+                )
+                prod = psum.tile([P, width], F32, name="prod", tag="prod", bufs=OUT_BANKS)
+                nc.tensor.matmul_mx(
+                    out=prod[:],
+                    lhsT=w2_codes[:].bitcast(FP8X4),
+                    lhsT_scale=w2_plane[:],
+                    rhs=z_codes[:].bitcast(FP8X4),
+                    rhs_scale=z_plane[:],
+                    start=True,
+                    stop=True,
+                )
+                result = ring.tile([P, width], F32, name="result", tag="result", bufs=4)
+                copy(out=result[:], in_=prod[:])
+                queue.dma_start(out=out[:, v0 + at : v0 + at + width], in_=result[:])
+
+        n0, n1, n2 = CHUNKS
+        z0 = sum_chunk(0, 0, n0)
+        second_product(0, n0, z0, nc.scalar.copy, nc.sync)
+
+        for d in range(LISTS):
+            late = ring.tile([P, BANK], F32, name=f"minus_gate1{d}", tag=f"w1_codes{2 + d}", align_bytes=64)
+            minus_gate[1].append(late)
+            nc.scalar.activation(out=late[:], in_=gate_late[d][:], func=ACT.Copy, scale=-1.0)
+
+        z1 = sum_chunk(1, n0, n1)
+        z2 = sum_chunk(2, n0 + n1, n2)
+        second_product(n0, n1, z1, nc.vector.tensor_copy, nc.sync)
+        second_product(n0 + n1, n2, z2, nc.scalar.copy, nc.scalar)

@@ -25,11 +25,14 @@ TILES = H // P
 LISTS = 2
 
 CHUNKS = (512, 384, 128)
-W1_LOADS = ((0, 128), (128, 128), (256, 256))
-VECTOR_ADD = (0, 2)
-BEHIND_QUANTISE = {(0, 1, 0): "w1_codes0", (0, 1, 1): "w1_codes1", (1, 1, 0): "z_packed0"}
+W1_LOADS = ((0, 128), (128, 128), (256, 128), (384, 128))
+VECTOR_ADD = None
+BEHIND_QUANTISE = {}
+AFTER_Z0 = (1, 2, 1)
 TERM_BUFS = 4
-SHORT_BANKS, SUM_BANKS, OUT_BANKS = 3, 3, 2
+PACKED_AT = (1536, 2048, 2048)
+SPREAD_BANKS = (6, 7)
+FIRST_BANKS = ((2, 3, 4, 5), (2, 3), (4, 5), (2, 3))
 
 
 def load_scale_rows(nc, plane, rows):
@@ -53,7 +56,12 @@ def tile_picked_wlapl_gelu_l_kernel(
     with ExitStack() as ctx:
         keep = ctx.enter_context(tc.tile_pool(name="keep", bufs=1))
         ring = ctx.enter_context(tc.tile_pool(name="ring", bufs=1))
+        head = ctx.enter_context(tc.tile_pool(name="head", bufs=1))
         psum = ctx.enter_context(tc.psum_pool(name="psum", bufs=1))
+
+        def bank(number, columns=BANK):
+            tile = psum.tile([P, columns], F32, name=f"bank{number}", tag=f"bank{number}")
+            return tile[:]
 
         x_plane = keep.tile([P, T], U8, align_bytes=64)
         w2_plane = keep.tile([P, N], U8, align_bytes=64)
@@ -63,12 +71,12 @@ def tile_picked_wlapl_gelu_l_kernel(
         nc.vector.memset(w2_plane[:].bitcast(I32), 0)
 
         w1_rows = w1.rearrange("(p j) c -> p j c", j=PACK)
-        w1_loaded = [keep.tile([P, PACK, cols], F32, name=f"w1_loaded{first}") for first, cols in W1_LOADS]
-        w1_raw = [w1_loaded[0][:], w1_loaded[1][:], w1_loaded[2][:, :, 0:P], w1_loaded[2][:, :, P : 2 * P]]
+        w1_loaded = [ring.tile([P, PACK, cols], F32, name=f"w1_loaded{first}", align_bytes=64) for first, cols in W1_LOADS]
+        w1_raw = [tile[:] for tile in w1_loaded]
         x_codes = [keep.tile([P, BANK], U32, name=f"x_codes{half}", align_bytes=64) for half in range(2)]
         x_bytes = x_words[0].rearrange("p n t -> p (n t)")
         gate_cols = keep.tile([P, LISTS, 4], F32)
-        gate_late = [keep.tile([P, BANK], F32, name=f"gate_late{d}") for d in range(LISTS)]
+        gate_late = keep.tile([P, LISTS, BANK], F32)
         lists = [keep.tile([P, T // LANES], U16, name=f"list{d}") for d in range(LISTS)]
         w2_codes = keep.tile([P, N], U32, align_bytes=64)
 
@@ -76,8 +84,8 @@ def tile_picked_wlapl_gelu_l_kernel(
             first, cols = W1_LOADS[i]
             nc.sync.dma_start(out=w1_loaded[i][:], in_=w1_rows[:, :, first : first + cols])
 
-        load_w1(0)
         nc.sync.dma_start(out=gate_cols[:], in_=gate[:, 0, 0:BANK].rearrange("d (n j) -> n d j", j=4))
+        load_w1(0)
         load_scale_rows(nc, x_plane, x_scales[0])
         for half in range(2):
             half_bytes = x_bytes[:, PACK * BANK * half : PACK * BANK * (half + 1)]
@@ -86,41 +94,46 @@ def tile_picked_wlapl_gelu_l_kernel(
         nc.sync.dma_start(lists[0][:], pos1)
         nc.sync.dma_start(lists[1][:], pos2)
         load_w1(2)
-        for d in range(LISTS):
-            nc.sync.dma_start(out=gate_late[d][:], in_=gate[d, :, BANK:T])
+        load_w1(3)
+        nc.sync.dma_start(out=gate_late[:], in_=gate[:, :, BANK:T].rearrange("d q v -> q d v"))
         nc.sync.dma_start(out=w2_codes[:].bitcast(I32), in_=w2_words[0].rearrange("p n t -> p (n t)").bitcast(I32))
         load_scale_rows(nc, w2_plane, w2_scales[0])
 
         nc.scalar.activation(out=warm[:, 1:2], in_=warm[:, 0:1], func=ACT.Gelu_apprx_tanh)
+        first_ident = ring.tile([P, P], F32, tag="w1_codes0", align_bytes=64)
+        make_identity(nc, first_ident[:])
         ident = keep.tile([P, P], F32)
         make_identity(nc, ident[:])
 
-        minus_gate = [[keep.tile([P, BANK], F32, name=f"minus_gate0{d}") for d in range(LISTS)], []]
+        minus_gate = [[], []]
 
         def spread_gate(d):
-            spread = psum.tile([P, 4, P], F32, name="spread", tag="short", bufs=SHORT_BANKS)
+            spread = bank(SPREAD_BANKS[d]).rearrange("q (j n) -> q j n", j=4)
             for j in range(4):
-                nc.tensor.transpose(spread[:, j, :], gate_cols[:, d, j : j + 1].to_broadcast([P, P]), ident[:])
-            nc.scalar.activation(
-                out=minus_gate[0][d][:].rearrange("q (n j) -> q n j", j=4),
-                in_=spread[:].rearrange("q j n -> q n j"),
-                func=ACT.Copy,
-                scale=-1.0,
+                nc.tensor.transpose(spread[:, j, :], gate_cols[:, d, j : j + 1].to_broadcast([P, P]), (first_ident, ident)[d][:])
+            return spread
+
+        def negate_gate(d, spread, tile):
+            minus_gate[0].append(tile)
+            nc.vector.tensor_scalar(
+                out=tile.rearrange("q (n j) -> q n j", j=4),
+                in0=spread.rearrange("q j n -> q n j"),
+                scalar1=-1.0,
+                scalar2=None,
+                op0=MULT,
             )
 
-        spread_gate(0)
+        spreads = [spread_gate(d) for d in range(LISTS)]
 
-        def quantise_w1(c, copy):
-            tag = f"w1_packed{c}" if c < 2 else f"w1_codes{c - 2}"
-            packed = ring.tile([P, P, PACK], BF16, name=f"w1_packed{c}", tag=tag, align_bytes=64)
+        def quantise_w1(c, copy, packed):
             copy(
-                out=packed[:].rearrange("p (m i) j -> p m j i", i=4),
+                out=packed.rearrange("p (m i) j -> p m j i", i=4),
                 in_=w1_raw[c].rearrange("p j (m i) -> p m j i", i=4),
             )
             codes = ring.tile([P, P], U32, name=f"w1_codes{c}", tag=f"w1_codes{c}", align_bytes=64)
             plane = keep.tile([P, P], U8, name=f"w1_plane{c}", align_bytes=64)
             nc.vector.quantize_mx(
-                out=codes[:].bitcast(FP8X4), scales=plane[:], in_=packed[:].rearrange("p m j -> p (m j)")
+                out=codes[:].bitcast(FP8X4), scales=plane[:], in_=packed.rearrange("p m j -> p (m j)")
             )
             return codes, plane
 
@@ -130,9 +143,9 @@ def tile_picked_wlapl_gelu_l_kernel(
             width = BANK // 2 if c == 0 else BANK
             for at in range(0, T, width):
                 cols = slice(at, at + width)
-                pre = psum.tile([P, width], F32, name="pre", tag="short", bufs=SHORT_BANKS)
+                pre = bank(FIRST_BANKS[c][at // width], width)
                 nc.tensor.matmul_mx(
-                    out=pre[:],
+                    out=pre,
                     lhsT=codes[:].bitcast(FP8X4),
                     lhsT_scale=plane[:],
                     rhs=x_codes[at // BANK][:, at % BANK : at % BANK + width].bitcast(FP8X4),
@@ -140,103 +153,146 @@ def tile_picked_wlapl_gelu_l_kernel(
                     start=True,
                     stop=True,
                 )
-                nc.scalar.activation(out=h[c][:, cols], in_=pre[:], func=ACT.Gelu_apprx_tanh)
+                nc.scalar.activation(out=h[c][:, cols], in_=pre, func=ACT.Gelu_apprx_tanh)
 
-        w1_mx = [quantise_w1(c, nc.vector.tensor_copy) for c in range(2)]
+        packed_first = head.tile([P, P, PACK], BF16, offset=3584, align_bytes=64)
+        w1_mx = [quantise_w1(0, nc.vector.tensor_copy, packed_first[:])]
+        early_gates = head.tile([P, LISTS, BANK], F32, offset=0, align_bytes=64)
+        for d in range(LISTS):
+            negate_gate(d, spreads[d], early_gates[:, d, :])
+        packed_second = head.tile([P, P, PACK], BF16, offset=4096, align_bytes=64)
+        w1_mx.append(quantise_w1(1, nc.vector.tensor_copy, packed_second[:]))
         for c in range(TILES):
             first_product(c, *w1_mx[c])
-            if c == 0:
-                spread_gate(1)
             if c < 2:
-                w1_mx.append(quantise_w1(c + 2, nc.scalar.copy))
+                packed = ring.tile([P, P, PACK], BF16, name=f"w1_packed{c + 2}", tag=f"w1_codes{c}", align_bytes=64)
+                w1_mx.append(quantise_w1(c + 2, nc.scalar.copy, packed[:]))
 
-        def sum_chunk(chunk, v0, n):
-            blocks = n // P
-            z_rows = ring.tile([P, blocks, 2, P, 2], BF16, name=f"z_rows{chunk}")
-            for c in range(TILES):
-                terms = []
-                for d in range(LISTS):
-                    if (chunk, c, d) in BEHIND_QUANTISE:
-                        term = ring.tile([P, n], F32, name="term_held", tag=BEHIND_QUANTISE[(chunk, c, d)], align_bytes=64)
-                    else:
-                        term = ring.tile([P, n], F32, name="term", tag="term", bufs=TERM_BUFS)
-                    nc.vector.tensor_tensor(
-                        term[:],
-                        h[c][:].indirect(lists[d][:, v0 // LANES : (v0 + n) // LANES]),
-                        minus_gate[v0 // BANK][d][:, v0 % BANK : v0 % BANK + n],
-                        MULT,
+        late_terms = []
+
+        def negate_late_gates():
+            late = ring.tile([P, LISTS, BANK], F32, name="minus_gate_late", tag="term020", align_bytes=64)
+            minus_gate[1].extend(late[:, d, :] for d in range(LISTS))
+            nc.scalar.activation(out=late[:], in_=gate_late[:], func=ACT.Copy, scale=-1.0)
+
+        starts = [sum(CHUNKS[:chunk]) for chunk in range(len(CHUNKS))]
+        z_rows = [ring.tile([P, n // P, 2, P, 2], BF16, name=f"z_rows{chunk}", align_bytes=64) for chunk, n in enumerate(CHUNKS)]
+        z_packed = {}
+
+        def gather(chunk, c, d):
+            v0, n = starts[chunk], CHUNKS[chunk]
+            if (chunk, c, d) in BEHIND_QUANTISE:
+                own = ring.tile([P, n], F32, name="term_held", tag=BEHIND_QUANTISE[(chunk, c, d)], align_bytes=64)
+                term = own[:]
+            elif (chunk, c, d) < AFTER_Z0:
+                own = ring.tile([P, n], F32, name=f"term{chunk}{c}{d}", align_bytes=64)
+                term = own[:]
+            else:
+                if not late_terms:
+                    late_terms.append(
+                        ring.tile([P, LISTS * TILES * BANK], F32, name="late_terms", tag="z_packed0", align_bytes=64)
                     )
-                    terms.append(term)
-                sums = psum.tile([P, blocks, P], F32, name="sums", tag="sum", bufs=SUM_BANKS)
-                parts = [h[c][:, v0 : v0 + n]] + [term[:] for term in terms]
-                if (chunk, c) == VECTOR_ADD:
-                    joined = ring.tile([P, n], F32, name="joined")
-                    nc.vector.tensor_tensor(joined[:], parts[0], parts[1], ADD)
-                    parts = [parts[2], joined[:]]
-                for i, part in enumerate(parts):
-                    for b in range(blocks):
-                        nc.tensor.matmul(
-                            sums[:, b, :],
-                            lhsT=part[:, b * P : (b + 1) * P],
-                            rhs=ident[:],
-                            start=(i == 0 and b == 0),
-                            stop=(i == len(parts) - 1 and b == blocks - 1),
-                            is_transpose=True,
-                        )
-                nc.scalar.copy(
-                    out=z_rows[:, :, :, 32 * c : 32 * (c + 1), :],
-                    in_=sums[:].rearrange("v b (p u e) -> v b u p e", u=2, e=2),
+                at = (LISTS * c + d) * BANK + v0 - BANK
+                term = late_terms[0][:, at : at + n]
+            nc.vector.tensor_tensor(
+                term,
+                h[c][:].indirect(lists[d][:, v0 // LANES : (v0 + n) // LANES]),
+                minus_gate[v0 // BANK][d][:, v0 % BANK : v0 % BANK + n],
+                MULT,
+            )
+            return term
+
+        def sum_tiles(chunk, tiles, sums, between=None):
+            v0, n = starts[chunk], CHUNKS[chunk]
+            blocks = n // P
+            sums = sums.rearrange("v (b m) -> v b m", b=blocks)
+            parts = [(i, h[c][:, v0 : v0 + n]) for i, c in enumerate(tiles)]
+            parts = parts + [(i, gather(chunk, c, d)) for i, c in enumerate(tiles) for d in range(LISTS)]
+            for k, (i, part) in enumerate(parts):
+                if between is not None and k == len(tiles):
+                    between()
+                for b in range(blocks):
+                    nc.tensor.matmul(
+                        sums[:, b, i * P : (i + 1) * P],
+                        lhsT=part[:, b * P : (b + 1) * P],
+                        rhs=ident[:],
+                        start=(k == 0 and b == 0),
+                        stop=(k == len(parts) - 1 and b == blocks - 1),
+                        is_transpose=True,
+                    )
+            nc.scalar.copy(
+                out=z_rows[chunk][:, :, :, 32 * tiles[0] : 32 * (tiles[-1] + 1), :],
+                in_=sums.rearrange("v b (p u e) -> v b u p e", u=2, e=2),
+            )
+
+        def turn_back(chunk, b0, nb, back, alone=True):
+            pairs = z_rows[chunk][:].rearrange("v b u p e -> v (b u p e)").bitcast(F32)
+            back = back.rearrange("p (b u v) -> p b u v", b=nb, u=2)
+            for b in range(nb):
+                for u in range(2):
+                    at = (2 * (b0 + b) + u) * P
+                    nc.tensor.matmul(
+                        back[:, b, u, :],
+                        lhsT=pairs[:, at : at + P],
+                        rhs=ident[:],
+                        start=alone,
+                        stop=alone,
+                        is_transpose=True,
+                    )
+            return back
+
+        def interleave(chunk, b0, nb, back, copy):
+            if chunk not in z_packed:
+                z_packed[chunk] = ring.tile(
+                    [P, CHUNKS[chunk], PACK], BF16, name=f"z_packed{chunk}", tag=f"z_packed{chunk}", align_bytes=64
                 )
+            z_words = z_packed[chunk][:].rearrange("p v t -> p (v t)").bitcast(F32)
+            copy(
+                out=z_words[:, 2 * P * b0 : 2 * P * (b0 + nb)].rearrange("p (b v u) -> p b v u", b=nb, u=2),
+                in_=back.rearrange("p b u v -> p b v u"),
+            )
 
-            z_packed = ring.tile([P, n, PACK], BF16, name=f"z_packed{chunk}", tag=f"z_packed{chunk}", align_bytes=64)
-            z_words = z_packed[:].rearrange("p v t -> p (v t)").bitcast(F32)
-            pairs = z_rows[:].rearrange("v b u p e -> v (b u p e)").bitcast(F32)
-            for b0 in range(0, blocks, 2):
-                nb = min(2, blocks - b0)
-                back = psum.tile([P, nb, 2, P], F32, name="back", tag="short", bufs=SHORT_BANKS)
-                for b in range(b0, b0 + nb):
-                    for u in range(2):
-                        at = (2 * b + u) * P
-                        nc.tensor.transpose(back[:, b - b0, u, :], pairs[:, at : at + P], ident[:])
-                nc.scalar.copy(
-                    out=z_words[:, 2 * P * b0 : 2 * P * (b0 + nb)].rearrange("p (b v u) -> p b v u", b=nb, u=2),
-                    in_=back[:].rearrange("p b u v -> p b v u"),
-                )
-            return z_packed
+        def second_product(chunk, at, width, prod, copy, queue):
+            v0 = starts[chunk] + at
+            z_codes = ring.tile([P, width], U32, name=f"z_codes{v0}", align_bytes=64)
+            z_plane = ring.tile([P, width], U8, name=f"z_plane{v0}", align_bytes=64)
+            nc.vector.quantize_mx(
+                out=z_codes[:].bitcast(FP8X4),
+                scales=z_plane[:],
+                in_=z_packed[chunk][:, at : at + width, :].rearrange("p v t -> p (v t)"),
+            )
+            nc.tensor.matmul_mx(
+                out=prod,
+                lhsT=w2_codes[:].bitcast(FP8X4),
+                lhsT_scale=w2_plane[:],
+                rhs=z_codes[:].bitcast(FP8X4),
+                rhs_scale=z_plane[:],
+                start=True,
+                stop=True,
+            )
+            result = ring.tile([P, width], F32, name=f"result{v0}")
+            copy(out=result[:], in_=prod)
+            queue.dma_start(out=out[:, v0 : v0 + width], in_=result[:])
 
-        def second_product(v0, n, z_packed, copy, queue):
-            for at, width in mx_pieces(n):
-                z_codes = ring.tile([P, width], U32, name="z_codes", tag="z_codes", bufs=4, align_bytes=64)
-                z_plane = ring.tile([P, width], U8, name="z_plane", tag="z_plane", bufs=4, align_bytes=64)
-                nc.vector.quantize_mx(
-                    out=z_codes[:].bitcast(FP8X4),
-                    scales=z_plane[:],
-                    in_=z_packed[:, at : at + width, :].rearrange("p v t -> p (v t)"),
-                )
-                prod = psum.tile([P, width], F32, name="prod", tag="prod", bufs=OUT_BANKS)
-                nc.tensor.matmul_mx(
-                    out=prod[:],
-                    lhsT=w2_codes[:].bitcast(FP8X4),
-                    lhsT_scale=w2_plane[:],
-                    rhs=z_codes[:].bitcast(FP8X4),
-                    rhs_scale=z_plane[:],
-                    start=True,
-                    stop=True,
-                )
-                result = ring.tile([P, width], F32, name="result", tag="result", bufs=4)
-                copy(out=result[:], in_=prod[:])
-                queue.dma_start(out=out[:, v0 + at : v0 + at + width], in_=result[:])
+        scalar_copy, vector_copy = nc.scalar.copy, nc.vector.tensor_copy
+        for c in range(TILES):
+            sum_tiles(0, [c], bank(c % 2))
+            if c == 2:
+                negate_late_gates()
+        interleave(0, 0, 2, turn_back(0, 0, 2, bank(5)), scalar_copy)
+        interleave(0, 2, 2, turn_back(0, 2, 2, bank(2)), scalar_copy)
+        second_product(0, 0, BANK, bank(7), scalar_copy, nc.sync)
 
-        n0, n1, n2 = CHUNKS
-        z0 = sum_chunk(0, 0, n0)
-        second_product(0, n0, z0, nc.scalar.copy, nc.sync)
-
-        for d in range(LISTS):
-            late = ring.tile([P, BANK], F32, name=f"minus_gate1{d}", tag=f"w1_codes{2 + d}", align_bytes=64)
-            minus_gate[1].append(late)
-            nc.scalar.activation(out=late[:], in_=gate_late[d][:], func=ACT.Copy, scale=-1.0)
-
-        z1 = sum_chunk(1, n0, n1)
-        z2 = sum_chunk(2, n0 + n1, n2)
-        second_product(n0, n1, z1, nc.vector.tensor_copy, nc.sync)
-        second_product(n0 + n1, n2, z2, nc.scalar.copy, nc.scalar)
+        for c, number in enumerate((0, 5, 2, 1)):
+            sum_tiles(1, [c], bank(number, CHUNKS[1]))
+        sum_tiles(2, [0], bank(0, P))
+        sum_tiles(2, [1], bank(5, P))
+        interleave(1, 0, 2, turn_back(1, 0, 2, bank(3)), scalar_copy)
+        shared = bank(4)
+        back = shared[:, 0 : 2 * P].rearrange("p (b u v) -> p b u v", b=1, u=2)
+        sum_tiles(2, [2, 3], shared[:, 2 * P : 4 * P], lambda: turn_back(1, 2, 1, shared[:, 0 : 2 * P], alone=False))
+        second_product(1, 0, 2 * P, bank(6, 2 * P), vector_copy, nc.sync)
+        interleave(1, 2, 1, back, vector_copy)
+        interleave(2, 0, 1, turn_back(2, 0, 1, bank(2, 2 * P)), scalar_copy)
+        second_product(1, 2 * P, P, bank(7, P), scalar_copy, nc.sync)
+        second_product(2, 0, P, bank(1, P), scalar_copy, nc.scalar)

@@ -27,8 +27,9 @@ LISTS = 2
 CHUNKS = (512, 384, 128)
 W1_LOADS = ((0, 128), (128, 128), (256, 128), (384, 128))
 VECTOR_ADD = None
-BEHIND_QUANTISE = {}
-AFTER_Z0 = (1, 2, 1)
+BEHIND_QUANTISE = {(1, 2, 0): 6080}
+Z_ROWS_AT = (2048, 2112, 8192)
+AFTER_Z0 = (1, 3, 0)
 TERM_BUFS = 4
 PACKED_AT = (1536, 2048, 2048)
 SPREAD_BANKS = (6, 7)
@@ -57,6 +58,7 @@ def tile_picked_wlapl_gelu_l_kernel(
         keep = ctx.enter_context(tc.tile_pool(name="keep", bufs=1))
         ring = ctx.enter_context(tc.tile_pool(name="ring", bufs=1))
         head = ctx.enter_context(tc.tile_pool(name="head", bufs=1))
+        laid = ctx.enter_context(tc.tile_pool(name="laid", bufs=1))
         psum = ctx.enter_context(tc.psum_pool(name="psum", bufs=1))
 
         def bank(number, columns=BANK):
@@ -155,6 +157,25 @@ def tile_picked_wlapl_gelu_l_kernel(
                 )
                 nc.scalar.activation(out=h[c][:, cols], in_=pre, func=ACT.Gelu_apprx_tanh)
 
+        fetched, scaled = {}, {}
+
+        def fetch_late(c):
+            fetched[c] = keep.tile([P, BANK], F32, name=f"fetched{c}")
+            nc.scalar.activation(
+                out=fetched[c][:], in_=h[c][:].indirect(lists[1][:, BANK // LANES : T // LANES]), func=ACT.Copy
+            )
+
+        def scale_late(c):
+            if c == 2:
+                scaled[c] = laid.tile([P, BANK], F32, name=f"scaled{c}", offset=64, align_bytes=64)
+            elif c == 1:
+                scaled[c] = ring.tile([P, BANK], F32, name=f"scaled{c}", tag="term031", align_bytes=64)
+            else:
+                scaled[c] = keep.tile([P, BANK], F32, name=f"scaled{c}")
+            nc.vector.scalar_tensor_tensor(
+                out=scaled[c][:], in0=fetched[c][:], scalar=-1.0, in1=gate_late[:, 1, :], op0=MULT, op1=MULT
+            )
+
         packed_first = head.tile([P, P, PACK], BF16, offset=3584, align_bytes=64)
         w1_mx = [quantise_w1(0, nc.vector.tensor_copy, packed_first[:])]
         early_gates = head.tile([P, LISTS, BANK], F32, offset=0, align_bytes=64)
@@ -162,27 +183,36 @@ def tile_picked_wlapl_gelu_l_kernel(
             negate_gate(d, spreads[d], early_gates[:, d, :])
         packed_second = head.tile([P, P, PACK], BF16, offset=4096, align_bytes=64)
         w1_mx.append(quantise_w1(1, nc.vector.tensor_copy, packed_second[:]))
-        for c in range(TILES):
+        for c in range(TILES - 1):
             first_product(c, *w1_mx[c])
             if c < 2:
                 packed = ring.tile([P, P, PACK], BF16, name=f"w1_packed{c + 2}", tag=f"w1_codes{c}", align_bytes=64)
                 w1_mx.append(quantise_w1(c + 2, nc.scalar.copy, packed[:]))
+            if c == 1:
+                fetch_late(0)
 
         late_terms = []
 
         def negate_late_gates():
-            late = ring.tile([P, LISTS, BANK], F32, name="minus_gate_late", tag="term020", align_bytes=64)
-            minus_gate[1].extend(late[:, d, :] for d in range(LISTS))
-            nc.scalar.activation(out=late[:], in_=gate_late[:], func=ACT.Copy, scale=-1.0)
+            late = ring.tile([P, BANK], F32, name="minus_gate_late", tag="term011", align_bytes=64)
+            minus_gate[1].append(late[:])
+            nc.scalar.activation(out=late[:], in_=gate_late[:, 0, :], func=ACT.Copy, scale=-1.0)
 
         starts = [sum(CHUNKS[:chunk]) for chunk in range(len(CHUNKS))]
-        z_rows = [ring.tile([P, n // P, 2, P, 2], BF16, name=f"z_rows{chunk}", align_bytes=64) for chunk, n in enumerate(CHUNKS)]
+        z_rows = [
+            laid.tile([P, n // P, 2, P, 2], BF16, name=f"z_rows{chunk}", offset=Z_ROWS_AT[chunk], align_bytes=64)
+            for chunk, n in enumerate(CHUNKS)
+        ]
         z_packed = {}
 
         def gather(chunk, c, d):
             v0, n = starts[chunk], CHUNKS[chunk]
+            if chunk > 0 and d == 1:
+                if c not in scaled:
+                    scale_late(c)
+                return scaled[c][:, v0 - BANK : v0 - BANK + n]
             if (chunk, c, d) in BEHIND_QUANTISE:
-                own = ring.tile([P, n], F32, name="term_held", tag=BEHIND_QUANTISE[(chunk, c, d)], align_bytes=64)
+                own = laid.tile([P, n], F32, name="term_held", offset=BEHIND_QUANTISE[(chunk, c, d)], align_bytes=64)
                 term = own[:]
             elif (chunk, c, d) < AFTER_Z0:
                 own = ring.tile([P, n], F32, name=f"term{chunk}{c}{d}", align_bytes=64)
@@ -207,7 +237,11 @@ def tile_picked_wlapl_gelu_l_kernel(
             blocks = n // P
             sums = sums.rearrange("v (b m) -> v b m", b=blocks)
             parts = [(i, h[c][:, v0 : v0 + n]) for i, c in enumerate(tiles)]
-            parts = parts + [(i, gather(chunk, c, d)) for i, c in enumerate(tiles) for d in range(LISTS)]
+            if chunk == 0:
+                parts = parts + [(i, gather(chunk, c, d)) for i, c in enumerate(tiles) for d in range(LISTS)]
+            else:
+                parts = parts + [(i, gather(chunk, c, d)) for i, c in reversed(list(enumerate(tiles))) for d in (1,)]
+                parts = parts + [(i, gather(chunk, c, 0)) for i, c in enumerate(tiles)]
             for k, (i, part) in enumerate(parts):
                 if between is not None and k == len(tiles):
                     between()
@@ -277,22 +311,24 @@ def tile_picked_wlapl_gelu_l_kernel(
         scalar_copy, vector_copy = nc.scalar.copy, nc.vector.tensor_copy
         for c in range(TILES):
             sum_tiles(0, [c], bank(c % 2))
-            if c == 2:
+            if c == 0:
+                fetch_late(1)
+                first_product(3, *w1_mx[3])
+            if c == 1:
                 negate_late_gates()
-        interleave(0, 0, 2, turn_back(0, 0, 2, bank(5)), scalar_copy)
-        interleave(0, 2, 2, turn_back(0, 2, 2, bank(2)), scalar_copy)
-        second_product(0, 0, BANK, bank(7), scalar_copy, nc.sync)
+            if c > 1:
+                fetch_late(c)
+        interleave(0, 0, 2, turn_back(0, 0, 2, bank(2)), scalar_copy)
+        interleave(0, 2, 2, turn_back(0, 2, 2, bank(3)), scalar_copy)
+        second_product(0, 0, BANK, bank(2), scalar_copy, nc.sync)
 
-        for c, number in enumerate((0, 5, 2, 1)):
+        for c, number in enumerate((6, 1, 4, 5)):
             sum_tiles(1, [c], bank(number, CHUNKS[1]))
-        sum_tiles(2, [0], bank(0, P))
-        sum_tiles(2, [1], bank(5, P))
+        sum_tiles(2, [0, 1, 2], bank(7, 3 * P))
+        sum_tiles(2, [3], bank(0, P))
         interleave(1, 0, 2, turn_back(1, 0, 2, bank(3)), scalar_copy)
-        shared = bank(4)
-        back = shared[:, 0 : 2 * P].rearrange("p (b u v) -> p b u v", b=1, u=2)
-        sum_tiles(2, [2, 3], shared[:, 2 * P : 4 * P], lambda: turn_back(1, 2, 1, shared[:, 0 : 2 * P], alone=False))
-        second_product(1, 0, 2 * P, bank(6, 2 * P), vector_copy, nc.sync)
-        interleave(1, 2, 1, back, vector_copy)
+        second_product(1, 0, 2 * P, bank(1, 2 * P), vector_copy, nc.sync)
+        interleave(1, 2, 1, turn_back(1, 2, 1, bank(6, 2 * P)), vector_copy)
         interleave(2, 0, 1, turn_back(2, 0, 1, bank(2, 2 * P)), scalar_copy)
-        second_product(1, 2 * P, P, bank(7, P), scalar_copy, nc.sync)
-        second_product(2, 0, P, bank(1, P), scalar_copy, nc.scalar)
+        second_product(1, 2 * P, P, bank(4, P), scalar_copy, nc.sync)
+        second_product(2, 0, P, bank(5, P), scalar_copy, nc.scalar)

@@ -68,8 +68,6 @@ def tile_picked_wlapl_gelu_l_kernel(
         x_plane = keep.tile([P, T], U8, align_bytes=64)
         w2_plane = keep.tile([P, N], U8, align_bytes=64)
         nc.gpsimd.memset(x_plane[:].bitcast(I32), 0)
-        warm = keep.tile([P, 2], F32)
-        nc.vector.memset(warm[:, 0:1], 0.0)
         nc.vector.memset(w2_plane[:].bitcast(I32), 0)
 
         w1_rows = w1.rearrange("(p j) c -> p j c", j=PACK)
@@ -101,7 +99,6 @@ def tile_picked_wlapl_gelu_l_kernel(
         nc.sync.dma_start(out=w2_codes[:].bitcast(I32), in_=w2_words[0].rearrange("p n t -> p (n t)").bitcast(I32))
         load_scale_rows(nc, w2_plane, w2_scales[0])
 
-        nc.scalar.activation(out=warm[:, 1:2], in_=warm[:, 0:1], func=ACT.Gelu_apprx_tanh)
         first_ident = ring.tile([P, P], F32, tag="w1_codes0", align_bytes=64)
         make_identity(nc, first_ident[:])
         ident = keep.tile([P, P], F32)

@@ -15,7 +15,7 @@ U8 = mybir.dt.uint8
 FP8X4 = mybir.dt.float8_e4m3fn_x4
 ACT = mybir.ActivationFunctionType
 MULT = mybir.AluOpType.mult
-ADD = mybir.AluOpType.add
+SUBTRACT = mybir.AluOpType.subtract
 
 P = 128
 PACK = 4
@@ -24,30 +24,20 @@ LANES = 16
 TILES = H // P
 LISTS = 2
 
-CHUNKS = (512, 384, 128)
 W1_LOADS = ((0, 128), (128, 128), (256, 128), (384, 128))
-VECTOR_ADD = None
-BEHIND_QUANTISE = {(1, 2, 0): 6080}
-Z_ROWS_AT = (2048, 2112, 8192)
-AFTER_Z0 = (1, 3, 0)
-TERM_BUFS = 4
-PACKED_AT = (1536, 2048, 2048)
 SPREAD_BANKS = (6, 7)
 FIRST_BANKS = ((2, 3, 4, 5), (2, 3), (4, 5), (2, 3))
+EARLY_SUM_BANKS = (0, 1, 6, 7)
+LATE_SUM_BANKS = (4, 5, 2, 3)
+FUSED = 256
+TERM_AT = {(0, 1, 0): 26624, (1, 1, 0): 28672}
+DEALT = 256
+LATE_BLOCKS = 2
 
 
 def load_scale_rows(nc, plane, rows):
     for q in range(4):
         nc.sync.dma_start(out=plane[32 * q : 32 * q + 4, :].bitcast(I32), in_=rows[4 * q : 4 * q + 4, :].bitcast(I32))
-
-
-def mx_pieces(n):
-    pieces, at = [], 0
-    for width in (512, 256, 128):
-        if n - at >= width:
-            pieces.append((at, width))
-            at = at + width
-    return pieces
 
 
 def tile_picked_wlapl_gelu_l_kernel(
@@ -71,7 +61,10 @@ def tile_picked_wlapl_gelu_l_kernel(
         nc.vector.memset(w2_plane[:].bitcast(I32), 0)
 
         w1_rows = w1.rearrange("(p j) c -> p j c", j=PACK)
-        w1_loaded = [ring.tile([P, PACK, cols], F32, name=f"w1_loaded{first}", align_bytes=64) for first, cols in W1_LOADS]
+        w1_loaded = [ring.tile([P, PACK, P], F32, name=f"w1_loaded{c}", align_bytes=64) for c in range(2)]
+        w1_loaded = w1_loaded + [
+            laid.tile([P, PACK, P], F32, name=f"w1_loaded{c}", offset=TERM_AT[(c - 2, 1, 0)], align_bytes=64) for c in (2, 3)
+        ]
         w1_raw = [tile[:] for tile in w1_loaded]
         x_codes = [keep.tile([P, BANK], U32, name=f"x_codes{half}", align_bytes=64) for half in range(2)]
         x_bytes = x_words[0].rearrange("p n t -> p (n t)")
@@ -104,7 +97,7 @@ def tile_picked_wlapl_gelu_l_kernel(
         ident = keep.tile([P, P], F32)
         make_identity(nc, ident[:])
 
-        minus_gate = [[], []]
+        minus_gate = []
 
         def spread_gate(d):
             spread = bank(SPREAD_BANKS[d]).rearrange("q (j n) -> q j n", j=4)
@@ -113,7 +106,7 @@ def tile_picked_wlapl_gelu_l_kernel(
             return spread
 
         def negate_gate(d, spread, tile):
-            minus_gate[0].append(tile)
+            minus_gate.append(tile)
             nc.vector.tensor_scalar(
                 out=tile.rearrange("q (n j) -> q n j", j=4),
                 in0=spread.rearrange("q j n -> q n j"),
@@ -129,8 +122,14 @@ def tile_picked_wlapl_gelu_l_kernel(
                 out=packed.rearrange("p (m i) j -> p m j i", i=4),
                 in_=w1_raw[c].rearrange("p j (m i) -> p m j i", i=4),
             )
-            codes = ring.tile([P, P], U32, name=f"w1_codes{c}", tag=f"w1_codes{c}", align_bytes=64)
-            plane = keep.tile([P, P], U8, name=f"w1_plane{c}", align_bytes=64)
+            if c in (1, 3):
+                codes = laid.tile([P, P], U32, name=f"w1_codes{c}", offset={1: 22528, 3: 2816}[c], align_bytes=64)
+            else:
+                codes = ring.tile([P, P], U32, name=f"w1_codes{c}", tag=f"w1_codes{c}", align_bytes=64)
+            if c == 3:
+                plane = laid.tile([P, P], U8, name="w1_plane3", offset=14336 - 64, align_bytes=64)
+            else:
+                plane = keep.tile([P, P], U8, name=f"w1_plane{c}", align_bytes=64)
             nc.vector.quantize_mx(
                 out=codes[:].bitcast(FP8X4), scales=plane[:], in_=packed.rearrange("p m j -> p (m j)")
             )
@@ -140,6 +139,7 @@ def tile_picked_wlapl_gelu_l_kernel(
 
         def first_product(c, codes, plane):
             width = BANK // 2 if c == 0 else BANK
+            pres = []
             for at in range(0, T, width):
                 cols = slice(at, at + width)
                 pre = bank(FIRST_BANKS[c][at // width], width)
@@ -152,146 +152,82 @@ def tile_picked_wlapl_gelu_l_kernel(
                     start=True,
                     stop=True,
                 )
+                pres.append((cols, pre))
+            return pres
+
+        def gelu(c, pres):
+            for cols, pre in pres:
                 nc.scalar.activation(out=h[c][:, cols], in_=pre, func=ACT.Gelu_apprx_tanh)
+            deal_h(c)
 
-        fetched, scaled = {}, {}
+        def gathered(c, d, v0, n):
+            return h[c][:].indirect(lists[d][:, v0 // LANES : (v0 + n) // LANES])
 
-        def fetch_late(c):
-            fetched[c] = keep.tile([P, BANK], F32, name=f"fetched{c}")
-            nc.scalar.activation(
-                out=fetched[c][:], in_=h[c][:].indirect(lists[1][:, BANK // LANES : T // LANES]), func=ACT.Copy
-            )
+        dealt_h = keep.tile([P, PACK, DEALT], F32)
+        dealt_plain = laid.tile([P, PACK, LISTS, DEALT], F32, offset=32768, align_bytes=64)
 
-        def scale_late(c):
-            if c == 2:
-                scaled[c] = laid.tile([P, BANK], F32, name=f"scaled{c}", offset=64, align_bytes=64)
-            elif c == 1:
-                scaled[c] = ring.tile([P, BANK], F32, name=f"scaled{c}", tag="term031", align_bytes=64)
+        def fetch(c, d, v0, plain):
+            nc.scalar.activation(out=plain, in_=gathered(c, d, v0, DEALT), func=ACT.Copy)
+
+        def scale(scaled, plain, gates):
+            nc.vector.scalar_tensor_tensor(out=scaled, in0=plain, scalar=-1.0, in1=gates, op0=MULT, op1=MULT)
+
+        def deal_plain(c):
+            for t in range(PACK):
+                nc.sync.dma_start(out=dealt_plain[32 * c : 32 * c + 32, t, :, :], in_=plain[c][t:P:PACK])
+
+        def deal_h(c):
+            for t in range(PACK):
+                nc.sync.dma_start(out=dealt_h[32 * c : 32 * c + 32, t, :], in_=h[c][t:P:PACK, T - DEALT : T])
+
+        def fused(c, d, v0, n, gates):
+            if (c, d, v0) in TERM_AT:
+                term = laid.tile([P, n], F32, name=f"term{c}_{d}_{v0}", offset=TERM_AT[(c, d, v0)], align_bytes=64)
             else:
-                scaled[c] = keep.tile([P, BANK], F32, name=f"scaled{c}")
-            nc.vector.scalar_tensor_tensor(
-                out=scaled[c][:], in0=fetched[c][:], scalar=-1.0, in1=gate_late[:, 1, :], op0=MULT, op1=MULT
-            )
+                term = keep.tile([P, n], F32, name=f"term{c}_{d}_{v0}")
+            nc.vector.tensor_tensor(term[:], gathered(c, d, v0, n), gates, MULT)
+            return term[:]
 
-        packed_first = head.tile([P, P, PACK], BF16, offset=3584, align_bytes=64)
-        w1_mx = [quantise_w1(0, nc.vector.tensor_copy, packed_first[:])]
-        early_gates = head.tile([P, LISTS, BANK], F32, offset=0, align_bytes=64)
-        for d in range(LISTS):
-            negate_gate(d, spreads[d], early_gates[:, d, :])
-        packed_second = head.tile([P, P, PACK], BF16, offset=4096, align_bytes=64)
-        w1_mx.append(quantise_w1(1, nc.vector.tensor_copy, packed_second[:]))
-        for c in range(TILES - 1):
-            first_product(c, *w1_mx[c])
-            if c < 2:
-                packed = ring.tile([P, P, PACK], BF16, name=f"w1_packed{c + 2}", tag=f"w1_codes{c}", align_bytes=64)
-                w1_mx.append(quantise_w1(c + 2, nc.scalar.copy, packed[:]))
-            if c == 1:
-                fetch_late(0)
+        def add_turned(sums, parts, first, last):
+            for k, (b, part) in enumerate(parts):
+                nc.tensor.matmul(
+                    sums[:, b * P : (b + 1) * P],
+                    lhsT=part,
+                    rhs=ident[:],
+                    start=(first and k == 0),
+                    stop=(last and k == len(parts) - 1),
+                    is_transpose=True,
+                )
 
-        late_terms = []
+        def blocks_of(tile, count, first=0):
+            return [(b, tile[:, (first + b) * P : (first + b + 1) * P]) for b in range(count)]
 
-        def negate_late_gates():
-            late = ring.tile([P, BANK], F32, name="minus_gate_late", tag="term011", align_bytes=64)
-            minus_gate[1].append(late[:])
-            nc.scalar.activation(out=late[:], in_=gate_late[:, 0, :], func=ACT.Copy, scale=-1.0)
+        z_early = laid.tile([P, BANK // P, 2, P, 2], BF16, offset=14336, align_bytes=64)
+        z_late = keep.tile([P, LATE_BLOCKS, 2, P, 2], BF16, align_bytes=64)
 
-        starts = [sum(CHUNKS[:chunk]) for chunk in range(len(CHUNKS))]
-        z_rows = [
-            laid.tile([P, n // P, 2, P, 2], BF16, name=f"z_rows{chunk}", offset=Z_ROWS_AT[chunk], align_bytes=64)
-            for chunk, n in enumerate(CHUNKS)
-        ]
-        z_packed = {}
+        def round_sums(rows, c, sums, copy):
+            copy(out=rows[:, :, :, 32 * c : 32 * (c + 1), :], in_=sums.rearrange("v (b p u e) -> v b u p e", p=32, u=2, e=2))
 
-        def gather(chunk, c, d):
-            v0, n = starts[chunk], CHUNKS[chunk]
-            if chunk > 0 and d == 1:
-                if c not in scaled:
-                    scale_late(c)
-                return scaled[c][:, v0 - BANK : v0 - BANK + n]
-            if (chunk, c, d) in BEHIND_QUANTISE:
-                own = laid.tile([P, n], F32, name="term_held", offset=BEHIND_QUANTISE[(chunk, c, d)], align_bytes=64)
-                term = own[:]
-            elif (chunk, c, d) < AFTER_Z0:
-                own = ring.tile([P, n], F32, name=f"term{chunk}{c}{d}", align_bytes=64)
-                term = own[:]
-            else:
-                if not late_terms:
-                    late_terms.append(
-                        ring.tile([P, LISTS * TILES * BANK], F32, name="late_terms", tag="z_packed0", align_bytes=64)
-                    )
-                at = (LISTS * c + d) * BANK + v0 - BANK
-                term = late_terms[0][:, at : at + n]
-            nc.vector.tensor_tensor(
-                term,
-                h[c][:].indirect(lists[d][:, v0 // LANES : (v0 + n) // LANES]),
-                minus_gate[v0 // BANK][d][:, v0 % BANK : v0 % BANK + n],
-                MULT,
-            )
-            return term
-
-        def sum_tiles(chunk, tiles, sums, between=None):
-            v0, n = starts[chunk], CHUNKS[chunk]
-            blocks = n // P
-            sums = sums.rearrange("v (b m) -> v b m", b=blocks)
-            parts = [(i, h[c][:, v0 : v0 + n]) for i, c in enumerate(tiles)]
-            if chunk == 0:
-                parts = parts + [(i, gather(chunk, c, d)) for i, c in enumerate(tiles) for d in range(LISTS)]
-            else:
-                parts = parts + [(i, gather(chunk, c, d)) for i, c in reversed(list(enumerate(tiles))) for d in (1,)]
-                parts = parts + [(i, gather(chunk, c, 0)) for i, c in enumerate(tiles)]
-            for k, (i, part) in enumerate(parts):
-                if between is not None and k == len(tiles):
-                    between()
-                for b in range(blocks):
-                    nc.tensor.matmul(
-                        sums[:, b, i * P : (i + 1) * P],
-                        lhsT=part[:, b * P : (b + 1) * P],
-                        rhs=ident[:],
-                        start=(k == 0 and b == 0),
-                        stop=(k == len(parts) - 1 and b == blocks - 1),
-                        is_transpose=True,
-                    )
-            nc.scalar.copy(
-                out=z_rows[chunk][:, :, :, 32 * tiles[0] : 32 * (tiles[-1] + 1), :],
-                in_=sums.rearrange("v b (p u e) -> v b u p e", u=2, e=2),
-            )
-
-        def turn_back(chunk, b0, nb, back, alone=True):
-            pairs = z_rows[chunk][:].rearrange("v b u p e -> v (b u p e)").bitcast(F32)
+        def turn_back(rows, b0, nb, back):
+            pairs = rows[:].rearrange("v b u p e -> v (b u p e)").bitcast(F32)
             back = back.rearrange("p (b u v) -> p b u v", b=nb, u=2)
             for b in range(nb):
                 for u in range(2):
                     at = (2 * (b0 + b) + u) * P
-                    nc.tensor.matmul(
-                        back[:, b, u, :],
-                        lhsT=pairs[:, at : at + P],
-                        rhs=ident[:],
-                        start=alone,
-                        stop=alone,
-                        is_transpose=True,
-                    )
+                    nc.tensor.transpose(back[:, b, u, :], pairs[:, at : at + P], ident[:])
             return back
 
-        def interleave(chunk, b0, nb, back, copy):
-            if chunk not in z_packed:
-                z_packed[chunk] = ring.tile(
-                    [P, CHUNKS[chunk], PACK], BF16, name=f"z_packed{chunk}", tag=f"z_packed{chunk}", align_bytes=64
-                )
-            z_words = z_packed[chunk][:].rearrange("p v t -> p (v t)").bitcast(F32)
+        def interleave(z_packed, b0, nb, back, copy):
+            z_words = z_packed[:].rearrange("p v t -> p (v t)").bitcast(F32)
             copy(
                 out=z_words[:, 2 * P * b0 : 2 * P * (b0 + nb)].rearrange("p (b v u) -> p b v u", b=nb, u=2),
                 in_=back.rearrange("p b u v -> p b v u"),
             )
 
-        def second_product(chunk, at, width, prod, copy, queue):
-            v0 = starts[chunk] + at
-            z_codes = ring.tile([P, width], U32, name=f"z_codes{v0}", align_bytes=64)
-            z_plane = ring.tile([P, width], U8, name=f"z_plane{v0}", align_bytes=64)
-            nc.vector.quantize_mx(
-                out=z_codes[:].bitcast(FP8X4),
-                scales=z_plane[:],
-                in_=z_packed[chunk][:, at : at + width, :].rearrange("p v t -> p (v t)"),
-            )
+        def quantise_z(z_packed, codes, plane):
+            nc.vector.quantize_mx(out=codes.bitcast(FP8X4), scales=plane, in_=z_packed[:].rearrange("p v t -> p (v t)"))
+
+        def project(z_codes, z_plane, prod):
             nc.tensor.matmul_mx(
                 out=prod,
                 lhsT=w2_codes[:].bitcast(FP8X4),
@@ -301,31 +237,132 @@ def tile_picked_wlapl_gelu_l_kernel(
                 start=True,
                 stop=True,
             )
-            result = ring.tile([P, width], F32, name=f"result{v0}")
+            return prod
+
+        def second_product(z_packed, width, prod, at):
+            z_codes = laid.tile([P, width], U32, name=f"z_codes{at}", offset=at, align_bytes=64)
+            z_plane = keep.tile([P, width], U8, name=f"z_plane{at}", align_bytes=64)
+            quantise_z(z_packed, z_codes[:], z_plane[:])
+            return project(z_codes, z_plane, prod)
+
+        def store(v0, width, prod, copy, queue):
+            result = keep.tile([P, width], F32, name=f"result{v0}")
             copy(out=result[:], in_=prod)
             queue.dma_start(out=out[:, v0 : v0 + width], in_=result[:])
 
         scalar_copy, vector_copy = nc.scalar.copy, nc.vector.tensor_copy
-        for c in range(TILES):
-            sum_tiles(0, [c], bank(c % 2))
-            if c == 0:
-                fetch_late(1)
-                first_product(3, *w1_mx[3])
-            if c == 1:
-                negate_late_gates()
-            if c > 1:
-                fetch_late(c)
-        interleave(0, 0, 2, turn_back(0, 0, 2, bank(2)), scalar_copy)
-        interleave(0, 2, 2, turn_back(0, 2, 2, bank(3)), scalar_copy)
-        second_product(0, 0, BANK, bank(2), scalar_copy, nc.sync)
 
-        for c, number in enumerate((6, 1, 4, 5)):
-            sum_tiles(1, [c], bank(number, CHUNKS[1]))
-        sum_tiles(2, [0, 1, 2], bank(7, 3 * P))
-        sum_tiles(2, [3], bank(0, P))
-        interleave(1, 0, 2, turn_back(1, 0, 2, bank(3)), scalar_copy)
-        second_product(1, 0, 2 * P, bank(1, 2 * P), vector_copy, nc.sync)
-        interleave(1, 2, 1, turn_back(1, 2, 1, bank(6, 2 * P)), vector_copy)
-        interleave(2, 0, 1, turn_back(2, 0, 1, bank(2, 2 * P)), scalar_copy)
-        second_product(1, 2 * P, P, bank(4, P), scalar_copy, nc.sync)
-        second_product(2, 0, P, bank(5, P), scalar_copy, nc.scalar)
+        early = {}
+
+        def early_open(c):
+            early[c] = bank(EARLY_SUM_BANKS[c])
+            add_turned(early[c], blocks_of(h[c][:], 4), True, False)
+
+        def early_term(c, d):
+            add_turned(early[c], blocks_of(fused(c, d, 0, BANK, minus_gate[d]), 4), False, d == LISTS - 1)
+
+        def late_open(c, number, blocks):
+            sums = bank(number, len(blocks) * P)
+            add_turned(sums, [(i, h[c][:, BANK + b * P : BANK + (b + 1) * P]) for i, b in enumerate(blocks)], True, False)
+            return sums
+
+        packed_first = head.tile([P, P, PACK], BF16, offset=3584, align_bytes=64)
+        w1_mx = [quantise_w1(0, nc.vector.tensor_copy, packed_first[:])]
+        early_gates = head.tile([P, LISTS, BANK], F32, offset=0, align_bytes=64)
+        for d in range(LISTS):
+            negate_gate(d, spreads[d], early_gates[:, d, :])
+        packed_second = head.tile([P, P, PACK], BF16, offset=4096, align_bytes=64)
+        w1_mx.append(quantise_w1(1, nc.vector.tensor_copy, packed_second[:]))
+
+        def scalar_weights(c):
+            if c == 2:
+                packed = ring.tile([P, P, PACK], BF16, name="w1_packed2", tag="w1_codes0", align_bytes=64)
+            else:
+                packed = laid.tile([P, P, PACK], BF16, name="w1_packed3", offset=21760, align_bytes=64)
+            w1_mx.append(quantise_w1(c, nc.scalar.copy, packed[:]))
+
+        both = (0, 1)
+        plain = [
+            laid.tile([P, LISTS, DEALT], F32, name=f"plain{c}", offset=(22784, 1024, 3072)[c], align_bytes=64)
+            for c in range(3)
+        ]
+        plain.append(keep.tile([P, LISTS, DEALT], F32, name="plain3"))
+
+        gelu(0, first_product(0, *w1_mx[0]))
+        scalar_weights(2)
+        gelu(1, first_product(1, *w1_mx[1]))
+        early_open(0)
+        pre2 = first_product(2, *w1_mx[2])
+        early_term(0, 0)
+        early_open(1)
+        early_term(0, 1)
+        scalar_weights(3)
+        pre3 = first_product(3, *w1_mx[3])
+        fetch(0, 0, T - DEALT, plain[0][:, 0, :])
+        gelu(2, pre2)
+        fetch(0, 1, T - DEALT, plain[0][:, 1, :])
+        deal_plain(0)
+        gelu(3, pre3)
+        minus_late = laid.tile([P, FUSED], F32, offset=14336 - 1024, align_bytes=64)
+        nc.scalar.activation(out=minus_late[:], in_=gate_late[:, 0, 0:FUSED], func=ACT.Copy, scale=-1.0)
+        for c in range(1, TILES):
+            for d in range(LISTS):
+                fetch(c, d, T - DEALT, plain[c][:, d, :])
+            deal_plain(c)
+        early_term(1, 0)
+        early_open(2)
+        early_term(1, 1)
+        early_open(3)
+        early_term(2, 0)
+        late = [late_open(c, LATE_SUM_BANKS[c], both) for c in range(2)]
+        early_term(2, 1)
+        late = late + [late_open(c, LATE_SUM_BANKS[c], both) for c in range(2, TILES)]
+        early_term(3, 0)
+        early_term(3, 1)
+        for c in range(TILES):
+            add_turned(late[c], blocks_of(fused(c, 0, BANK, FUSED, minus_late[:]), 2), False, False)
+        plain_late = keep.tile([P, TILES, FUSED], F32)
+        scaled_late = keep.tile([P, TILES, FUSED], F32)
+        for c in range(TILES):
+            fetch(c, 1, BANK, plain_late[:, c, :])
+            scale(scaled_late[:, c, :], plain_late[:, c, :], gate_late[:, 1, 0:FUSED])
+            add_turned(late[c], blocks_of(scaled_late[:, c, :], 2), False, True)
+        for c in range(TILES):
+            round_sums(z_early, c, early[c], scalar_copy)
+        back_early = [turn_back(z_early, 2 * i, 2, bank(i)) for i in range(2)]
+        for c in range(TILES):
+            round_sums(z_late, c, late[c], scalar_copy)
+        packed = [keep.tile([P, 2 * P, PACK], BF16, name=f"z_packed{i}", align_bytes=64) for i in range(4)]
+        for i in range(2):
+            interleave(packed[i], 0, 2, back_early[i], scalar_copy)
+        interleave(packed[2], 0, 2, turn_back(z_late, 0, 2, bank(6)), scalar_copy)
+
+        dealt_terms = [
+            laid.tile([P, PACK, DEALT], F32, name=f"dealt_term{d}", offset=(6144, 18432)[d], align_bytes=64)
+            for d in range(LISTS)
+        ]
+        for d in range(LISTS):
+            gates = gate_late[:, d, FUSED:].unsqueeze(1).to_broadcast([P, PACK, DEALT])
+            nc.vector.tensor_tensor(dealt_terms[d][:], dealt_plain[:, :, d, :], gates, MULT)
+        less_first = keep.tile([P, PACK, DEALT], F32)
+        nc.vector.tensor_tensor(less_first[:], dealt_h[:], dealt_terms[0][:], SUBTRACT)
+
+        def finish_dealt(block):
+            cols = slice(block * P, (block + 1) * P)
+            nc.vector.tensor_tensor(
+                packed[3][:, cols, :].rearrange("p (m i) j -> p m j i", i=4),
+                less_first[:, :, cols].rearrange("p j (m i) -> p m j i", i=4),
+                dealt_terms[1][:, :, cols].rearrange("p j (m i) -> p m j i", i=4),
+                SUBTRACT,
+            )
+
+        prods = [second_product(packed[0], 2 * P, bank(7, 2 * P), 32768)]
+        finish_dealt(0)
+        prods.append(second_product(packed[1], 2 * P, bank(4, 2 * P), 6144))
+        finish_dealt(1)
+        prods.append(second_product(packed[2], 2 * P, bank(5, 2 * P), 7168))
+        prods.append(second_product(packed[3], 2 * P, bank(2, 2 * P), 8192))
+        store(0, 2 * P, prods[0], scalar_copy, nc.sync)
+        store(2 * P, 2 * P, prods[1], scalar_copy, nc.sync)
+        store(4 * P, 2 * P, prods[2], vector_copy, nc.sync)
+        store(6 * P, 2 * P, prods[3], scalar_copy, nc.scalar)

@@ -28,7 +28,8 @@ W1_LOADS = ((0, 128), (128, 128), (256, 128), (384, 128))
 SPREAD_BANKS = (6, 7)
 FIRST_BANKS = ((2, 3, 4, 5), (2, 3), (4, 5), (2, 3))
 EARLY_SUM_BANKS = (0, 1, 6, 7)
-LATE_SUM_BANKS = (4, 5, 2, 3)
+LATE_SUM_BANKS = (2, 3)
+DEALT_GATE_BANK = 4
 FUSED = 256
 TERM_AT = {(0, 1, 0): 26624, (1, 1, 0): 28672}
 DEALT = 256
@@ -69,7 +70,8 @@ def tile_picked_wlapl_gelu_l_kernel(
         x_codes = [keep.tile([P, BANK], U32, name=f"x_codes{half}", align_bytes=64) for half in range(2)]
         x_bytes = x_words[0].rearrange("p n t -> p (n t)")
         gate_cols = keep.tile([P, LISTS, 4], F32)
-        gate_late = keep.tile([P, LISTS, BANK], F32)
+        gate_late = keep.tile([P, LISTS, FUSED], F32)
+        dealt_cols = keep.tile([P, LISTS, 2], F32)
         lists = [keep.tile([P, T // LANES], U16, name=f"list{d}") for d in range(LISTS)]
         w2_codes = keep.tile([P, N], U32, align_bytes=64)
 
@@ -88,7 +90,8 @@ def tile_picked_wlapl_gelu_l_kernel(
         nc.sync.dma_start(lists[1][:], pos2)
         load_w1(2)
         load_w1(3)
-        nc.sync.dma_start(out=gate_late[:], in_=gate[:, :, BANK:T].rearrange("d q v -> q d v"))
+        nc.sync.dma_start(out=dealt_cols[:], in_=gate[:, 0, T - DEALT : T].rearrange("d (n j) -> n d j", j=2))
+        nc.sync.dma_start(out=gate_late[:], in_=gate[:, :, BANK : BANK + FUSED].rearrange("d q v -> q d v"))
         nc.sync.dma_start(out=w2_codes[:].bitcast(I32), in_=w2_words[0].rearrange("p n t -> p (n t)").bitcast(I32))
         load_scale_rows(nc, w2_plane, w2_scales[0])
 
@@ -205,8 +208,8 @@ def tile_picked_wlapl_gelu_l_kernel(
         z_early = laid.tile([P, BANK // P, 2, P, 2], BF16, offset=14336, align_bytes=64)
         z_late = keep.tile([P, LATE_BLOCKS, 2, P, 2], BF16, align_bytes=64)
 
-        def round_sums(rows, c, sums, copy):
-            copy(out=rows[:, :, :, 32 * c : 32 * (c + 1), :], in_=sums.rearrange("v (b p u e) -> v b u p e", p=32, u=2, e=2))
+        def round_sums(rows, c, sums, copy, width=32):
+            copy(out=rows[:, :, :, width * c : width * (c + 1), :], in_=sums.rearrange("v (b p u e) -> v b u p e", p=width, u=2, e=2))
 
         def turn_back(rows, b0, nb, back):
             pairs = rows[:].rearrange("v b u p e -> v (b u p e)").bitcast(F32)
@@ -261,10 +264,14 @@ def tile_picked_wlapl_gelu_l_kernel(
         def early_term(c, d):
             add_turned(early[c], blocks_of(fused(c, d, 0, BANK, minus_gate[d]), 4), False, d == LISTS - 1)
 
-        def late_open(c, number, blocks):
-            sums = bank(number, len(blocks) * P)
-            add_turned(sums, [(i, h[c][:, BANK + b * P : BANK + (b + 1) * P]) for i, b in enumerate(blocks)], True, False)
+        def late_open(pair):
+            sums = bank(LATE_SUM_BANKS[pair])
+            parts = [(2 * b + c % 2, h[c][:, BANK + b * P : BANK + (b + 1) * P]) for c in (2 * pair, 2 * pair + 1) for b in range(2)]
+            add_turned(sums, parts, True, False)
             return sums
+
+        def late_blocks(c, tile):
+            return [(2 * b + c % 2, part) for b, part in blocks_of(tile, 2)]
 
         packed_first = head.tile([P, P, PACK], BF16, offset=3584, align_bytes=64)
         w1_mx = [quantise_w1(0, nc.vector.tensor_copy, packed_first[:])]
@@ -281,7 +288,6 @@ def tile_picked_wlapl_gelu_l_kernel(
                 packed = laid.tile([P, P, PACK], BF16, name="w1_packed3", offset=21760, align_bytes=64)
             w1_mx.append(quantise_w1(c, nc.scalar.copy, packed[:]))
 
-        both = (0, 1)
         plain = [
             laid.tile([P, LISTS, DEALT], F32, name=f"plain{c}", offset=(22784, 1024, 3072)[c], align_bytes=64)
             for c in range(3)
@@ -310,28 +316,32 @@ def tile_picked_wlapl_gelu_l_kernel(
                 fetch(c, d, T - DEALT, plain[c][:, d, :])
             deal_plain(c)
         early_term(1, 0)
+        dealt_gate = bank(DEALT_GATE_BANK).rearrange("q (d j n) -> q d j n", d=LISTS, j=2)
+        for d in range(LISTS):
+            for j in range(2):
+                nc.tensor.transpose(dealt_gate[:, d, j, :], dealt_cols[:, d, j : j + 1].to_broadcast([P, P]), ident[:])
         early_open(2)
         early_term(1, 1)
         early_open(3)
         early_term(2, 0)
-        late = [late_open(c, LATE_SUM_BANKS[c], both) for c in range(2)]
+        late = [late_open(0)]
         early_term(2, 1)
-        late = late + [late_open(c, LATE_SUM_BANKS[c], both) for c in range(2, TILES)]
+        late = late + [late_open(1)]
         early_term(3, 0)
         early_term(3, 1)
         for c in range(TILES):
-            add_turned(late[c], blocks_of(fused(c, 0, BANK, FUSED, minus_late[:]), 2), False, False)
+            add_turned(late[c // 2], late_blocks(c, fused(c, 0, BANK, FUSED, minus_late[:])), False, False)
         plain_late = keep.tile([P, TILES, FUSED], F32)
         scaled_late = keep.tile([P, TILES, FUSED], F32)
         for c in range(TILES):
             fetch(c, 1, BANK, plain_late[:, c, :])
             scale(scaled_late[:, c, :], plain_late[:, c, :], gate_late[:, 1, 0:FUSED])
-            add_turned(late[c], blocks_of(scaled_late[:, c, :], 2), False, True)
+            add_turned(late[c // 2], late_blocks(c, scaled_late[:, c, :]), False, c % 2 == 1)
         for c in range(TILES):
             round_sums(z_early, c, early[c], scalar_copy)
         back_early = [turn_back(z_early, 2 * i, 2, bank(i)) for i in range(2)]
-        for c in range(TILES):
-            round_sums(z_late, c, late[c], scalar_copy)
+        for pair in range(2):
+            round_sums(z_late, pair, late[pair], scalar_copy, 64)
         packed = [keep.tile([P, 2 * P, PACK], BF16, name=f"z_packed{i}", align_bytes=64) for i in range(4)]
         for i in range(2):
             interleave(packed[i], 0, 2, back_early[i], scalar_copy)
@@ -341,11 +351,22 @@ def tile_picked_wlapl_gelu_l_kernel(
             laid.tile([P, PACK, DEALT], F32, name=f"dealt_term{d}", offset=(6144, 18432)[d], align_bytes=64)
             for d in range(LISTS)
         ]
-        for d in range(LISTS):
-            gates = gate_late[:, d, FUSED:].unsqueeze(1).to_broadcast([P, PACK, DEALT])
-            nc.vector.tensor_tensor(dealt_terms[d][:], dealt_plain[:, :, d, :], gates, MULT)
         less_first = keep.tile([P, PACK, DEALT], F32)
-        nc.vector.tensor_tensor(less_first[:], dealt_h[:], dealt_terms[0][:], SUBTRACT)
+
+        def dealt_product(d, n0, n1):
+            gates = dealt_gate[:, d, :, n0:n1].rearrange("q j n -> q n j").unsqueeze(1).to_broadcast([P, PACK, n1 - n0, 2])
+            nc.vector.tensor_tensor(
+                dealt_terms[d][:, :, 2 * n0 : 2 * n1].rearrange("p t (n j) -> p t n j", j=2),
+                dealt_plain[:, :, d, 2 * n0 : 2 * n1].rearrange("p t (n j) -> p t n j", j=2),
+                gates,
+                MULT,
+            )
+
+        dealt_product(0, 0, 64)
+        nc.gpsimd.tensor_tensor(less_first[:, :, 0:P], dealt_h[:, :, 0:P], dealt_terms[0][:, :, 0:P], SUBTRACT)
+        dealt_product(0, 64, P)
+        dealt_product(1, 0, P)
+        nc.vector.tensor_tensor(less_first[:, :, P:], dealt_h[:, :, P:], dealt_terms[0][:, :, P:], SUBTRACT)
 
         def finish_dealt(block):
             cols = slice(block * P, (block + 1) * P)
@@ -358,9 +379,9 @@ def tile_picked_wlapl_gelu_l_kernel(
 
         prods = [second_product(packed[0], 2 * P, bank(7, 2 * P), 32768)]
         finish_dealt(0)
-        prods.append(second_product(packed[1], 2 * P, bank(4, 2 * P), 6144))
+        prods.append(second_product(packed[1], 2 * P, bank(5, 2 * P), 6144))
         finish_dealt(1)
-        prods.append(second_product(packed[2], 2 * P, bank(5, 2 * P), 7168))
+        prods.append(second_product(packed[2], 2 * P, bank(3, 2 * P), 7168))
         prods.append(second_product(packed[3], 2 * P, bank(2, 2 * P), 8192))
         store(0, 2 * P, prods[0], scalar_copy, nc.sync)
         store(2 * P, 2 * P, prods[1], scalar_copy, nc.sync)

@@ -26,9 +26,9 @@ LISTS = 2
 
 W1_LOADS = ((0, 128), (128, 128), (256, 128), (384, 128))
 SPREAD_BANKS = (6, 7)
-FIRST_BANKS = ((2, 3, 4, 5), (2, 3), (4, 5), (2, 3))
+FIRST_BANKS = ((2, 3, 4, 5), (4, 5), (2, 3), (2, 3))
 EARLY_SUM_BANKS = (0, 1, 6, 7)
-LATE_SUM_BANKS = (2, 3)
+LATE_SUM_BANKS = (5, 2)
 DEALT_GATE_BANK = 4
 FUSED = 256
 TERM_AT = {(0, 1, 0): 26624, (1, 1, 0): 28672}
@@ -67,7 +67,7 @@ def tile_picked_wlapl_gelu_l_kernel(
             laid.tile([P, PACK, P], F32, name=f"w1_loaded{c}", offset=TERM_AT[(c - 2, 1, 0)], align_bytes=64) for c in (2, 3)
         ]
         w1_raw = [tile[:] for tile in w1_loaded]
-        x_codes = [keep.tile([P, BANK], U32, name=f"x_codes{half}", align_bytes=64) for half in range(2)]
+        x_codes = [laid.tile([P, BANK], U32, name=f"x_codes{half}", offset=45056 - 2048 * half, align_bytes=64) for half in range(2)]
         x_bytes = x_words[0].rearrange("p n t -> p (n t)")
         gate_cols = keep.tile([P, LISTS, 4], F32)
         gate_late = keep.tile([P, LISTS, FUSED], F32)
@@ -88,9 +88,9 @@ def tile_picked_wlapl_gelu_l_kernel(
         load_w1(1)
         nc.sync.dma_start(lists[0][:], pos1)
         nc.sync.dma_start(lists[1][:], pos2)
+        nc.sync.dma_start(out=dealt_cols[:], in_=gate[:, 0, T - DEALT : T].rearrange("d (n j) -> n d j", j=2))
         load_w1(2)
         load_w1(3)
-        nc.sync.dma_start(out=dealt_cols[:], in_=gate[:, 0, T - DEALT : T].rearrange("d (n j) -> n d j", j=2))
         nc.sync.dma_start(out=gate_late[:], in_=gate[:, :, BANK : BANK + FUSED].rearrange("d q v -> q d v"))
         nc.sync.dma_start(out=w2_codes[:].bitcast(I32), in_=w2_words[0].rearrange("p n t -> p (n t)").bitcast(I32))
         load_scale_rows(nc, w2_plane, w2_scales[0])
@@ -129,8 +129,8 @@ def tile_picked_wlapl_gelu_l_kernel(
                 codes = laid.tile([P, P], U32, name=f"w1_codes{c}", offset={1: 22528, 3: 2816}[c], align_bytes=64)
             else:
                 codes = ring.tile([P, P], U32, name=f"w1_codes{c}", tag=f"w1_codes{c}", align_bytes=64)
-            if c == 3:
-                plane = laid.tile([P, P], U8, name="w1_plane3", offset=14336 - 64, align_bytes=64)
+            if c >= 2:
+                plane = laid.tile([P, P], U8, name=f"w1_plane{c}", offset=14336 + P * (c - 3), align_bytes=64)
             else:
                 plane = keep.tile([P, P], U8, name=f"w1_plane{c}", align_bytes=64)
             nc.vector.quantize_mx(
@@ -301,37 +301,37 @@ def tile_picked_wlapl_gelu_l_kernel(
         pre2 = first_product(2, *w1_mx[2])
         early_term(0, 0)
         early_open(1)
-        early_term(0, 1)
-        scalar_weights(3)
-        pre3 = first_product(3, *w1_mx[3])
-        fetch(0, 0, T - DEALT, plain[0][:, 0, :])
-        gelu(2, pre2)
-        fetch(0, 1, T - DEALT, plain[0][:, 1, :])
-        deal_plain(0)
-        gelu(3, pre3)
-        minus_late = laid.tile([P, FUSED], F32, offset=14336 - 1024, align_bytes=64)
-        nc.scalar.activation(out=minus_late[:], in_=gate_late[:, 0, 0:FUSED], func=ACT.Copy, scale=-1.0)
-        for c in range(1, TILES):
-            for d in range(LISTS):
-                fetch(c, d, T - DEALT, plain[c][:, d, :])
-            deal_plain(c)
-        early_term(1, 0)
         dealt_gate = bank(DEALT_GATE_BANK).rearrange("q (d j n) -> q d j n", d=LISTS, j=2)
         for d in range(LISTS):
             for j in range(2):
                 nc.tensor.transpose(dealt_gate[:, d, j, :], dealt_cols[:, d, j : j + 1].to_broadcast([P, P]), ident[:])
+        late = [late_open(0)]
+        early_term(0, 1)
+        scalar_weights(3)
+        fetch(0, 0, T - DEALT, plain[0][:, 0, :])
+        gelu(2, pre2)
+        early_term(1, 0)
+        pre3 = first_product(3, *w1_mx[3])
+        fetch(0, 1, T - DEALT, plain[0][:, 1, :])
+        deal_plain(0)
+        minus_late = laid.tile([P, FUSED], F32, offset=14336 - 1024, align_bytes=64)
+        nc.scalar.activation(out=minus_late[:], in_=gate_late[:, 0, 0:FUSED], func=ACT.Copy, scale=-1.0)
+        gelu(3, pre3)
+        for c in range(1, TILES):
+            for d in range(LISTS):
+                fetch(c, d, T - DEALT, plain[c][:, d, :])
+            deal_plain(c)
         early_open(2)
         early_term(1, 1)
-        early_open(3)
         early_term(2, 0)
-        late = [late_open(0)]
-        early_term(2, 1)
+        early_open(3)
         late = late + [late_open(1)]
+        early_term(2, 1)
         early_term(3, 0)
         early_term(3, 1)
         for c in range(TILES):
             add_turned(late[c // 2], late_blocks(c, fused(c, 0, BANK, FUSED, minus_late[:])), False, False)
-        plain_late = keep.tile([P, TILES, FUSED], F32)
+        plain_late = laid.tile([P, TILES, FUSED], F32, offset=40960, align_bytes=64)
         scaled_late = keep.tile([P, TILES, FUSED], F32)
         for c in range(TILES):
             fetch(c, 1, BANK, plain_late[:, c, :])
@@ -351,7 +351,9 @@ def tile_picked_wlapl_gelu_l_kernel(
             laid.tile([P, PACK, DEALT], F32, name=f"dealt_term{d}", offset=(6144, 18432)[d], align_bytes=64)
             for d in range(LISTS)
         ]
-        less_first = keep.tile([P, PACK, DEALT], F32)
+        less_first = [
+            laid.tile([P, PACK, P], F32, name=f"less_first{b}", offset=47104 + 2048 * b, align_bytes=64) for b in range(2)
+        ]
 
         def dealt_product(d, n0, n1):
             gates = dealt_gate[:, d, :, n0:n1].rearrange("q j n -> q n j").unsqueeze(1).to_broadcast([P, PACK, n1 - n0, 2])
@@ -363,27 +365,27 @@ def tile_picked_wlapl_gelu_l_kernel(
             )
 
         dealt_product(0, 0, 64)
-        nc.gpsimd.tensor_tensor(less_first[:, :, 0:P], dealt_h[:, :, 0:P], dealt_terms[0][:, :, 0:P], SUBTRACT)
+        nc.gpsimd.tensor_tensor(less_first[0][:], dealt_h[:, :, 0:P], dealt_terms[0][:, :, 0:P], SUBTRACT)
         dealt_product(0, 64, P)
         dealt_product(1, 0, P)
-        nc.vector.tensor_tensor(less_first[:, :, P:], dealt_h[:, :, P:], dealt_terms[0][:, :, P:], SUBTRACT)
+        nc.vector.tensor_tensor(less_first[1][:], dealt_h[:, :, P:], dealt_terms[0][:, :, P:], SUBTRACT)
 
         def finish_dealt(block):
             cols = slice(block * P, (block + 1) * P)
             nc.vector.tensor_tensor(
                 packed[3][:, cols, :].rearrange("p (m i) j -> p m j i", i=4),
-                less_first[:, :, cols].rearrange("p j (m i) -> p m j i", i=4),
+                less_first[block][:].rearrange("p j (m i) -> p m j i", i=4),
                 dealt_terms[1][:, :, cols].rearrange("p j (m i) -> p m j i", i=4),
                 SUBTRACT,
             )
 
-        prods = [second_product(packed[0], 2 * P, bank(7, 2 * P), 32768)]
         finish_dealt(0)
-        prods.append(second_product(packed[1], 2 * P, bank(5, 2 * P), 6144))
         finish_dealt(1)
-        prods.append(second_product(packed[2], 2 * P, bank(3, 2 * P), 7168))
-        prods.append(second_product(packed[3], 2 * P, bank(2, 2 * P), 8192))
+        prods = {
+            i: second_product(packed[i], 2 * P, bank(number, 2 * P), at)
+            for i, number, at in ((0, 7, 47104), (3, 4, 50176), (1, 3, 48128), (2, 5, 49152))
+        }
         store(0, 2 * P, prods[0], scalar_copy, nc.sync)
-        store(2 * P, 2 * P, prods[1], scalar_copy, nc.sync)
-        store(4 * P, 2 * P, prods[2], vector_copy, nc.sync)
-        store(6 * P, 2 * P, prods[3], scalar_copy, nc.scalar)
+        store(6 * P, 2 * P, prods[3], scalar_copy, nc.sync)
+        store(2 * P, 2 * P, prods[1], vector_copy, nc.sync)
+        store(4 * P, 2 * P, prods[2], scalar_copy, nc.scalar)

@@ -31,7 +31,7 @@ EARLY_SUM_BANKS = (0, 1, 6, 7)
 LATE_SUM_BANKS = (5, 2)
 DEALT_GATE_BANK = 4
 FUSED = 256
-TERM_AT = {(0, 1, 0): 26624, (1, 1, 0): 28672}
+TERM_AT = {(0, 1, 0): 26624}
 DEALT = 256
 LATE_BLOCKS = 2
 
@@ -56,7 +56,7 @@ def tile_picked_wlapl_gelu_l_kernel(
             tile = psum.tile([P, columns], F32, name=f"bank{number}", tag=f"bank{number}")
             return tile[:]
 
-        x_plane = keep.tile([P, T], U8, align_bytes=64)
+        x_plane = laid.tile([P, T], U8, offset=16384, align_bytes=64)
         w2_plane = keep.tile([P, N], U8, align_bytes=64)
         nc.gpsimd.memset(x_plane[:].bitcast(I32), 0)
         nc.vector.memset(w2_plane[:].bitcast(I32), 0)
@@ -64,7 +64,7 @@ def tile_picked_wlapl_gelu_l_kernel(
         w1_rows = w1.rearrange("(p j) c -> p j c", j=PACK)
         w1_loaded = [ring.tile([P, PACK, P], F32, name=f"w1_loaded{c}", align_bytes=64) for c in range(2)]
         w1_loaded = w1_loaded + [
-            laid.tile([P, PACK, P], F32, name=f"w1_loaded{c}", offset=TERM_AT[(c - 2, 1, 0)], align_bytes=64) for c in (2, 3)
+            laid.tile([P, PACK, P], F32, name=f"w1_loaded{c}", offset=26624 + 2048 * (c - 2), align_bytes=64) for c in (2, 3)
         ]
         w1_raw = [tile[:] for tile in w1_loaded]
         x_codes = [laid.tile([P, BANK], U32, name=f"x_codes{half}", offset=45056 - 2048 * half, align_bytes=64) for half in range(2)]
@@ -120,13 +120,16 @@ def tile_picked_wlapl_gelu_l_kernel(
 
         spreads = [spread_gate(d) for d in range(LISTS)]
 
-        def quantise_w1(c, copy, packed):
+        def round_w1(c, copy, packed):
             copy(
                 out=packed.rearrange("p (m i) j -> p m j i", i=4),
                 in_=w1_raw[c].rearrange("p j (m i) -> p m j i", i=4),
             )
-            if c in (1, 3):
-                codes = laid.tile([P, P], U32, name=f"w1_codes{c}", offset={1: 22528, 3: 2816}[c], align_bytes=64)
+            return packed
+
+        def quantise_w1(c, packed):
+            if c > 0:
+                codes = laid.tile([P, P], U32, name=f"w1_codes{c}", offset={1: 22528, 2: 1024, 3: 3072}[c], align_bytes=64)
             else:
                 codes = ring.tile([P, P], U32, name=f"w1_codes{c}", tag=f"w1_codes{c}", align_bytes=64)
             if c >= 2:
@@ -205,7 +208,9 @@ def tile_picked_wlapl_gelu_l_kernel(
         def blocks_of(tile, count, first=0):
             return [(b, tile[:, (first + b) * P : (first + b + 1) * P]) for b in range(count)]
 
-        z_early = laid.tile([P, BANK // P, 2, P, 2], BF16, offset=14336, align_bytes=64)
+        z_early = [
+            laid.tile([P, 2, 2, P, 2], BF16, name=f"z_early{half}", offset=14336 + 2048 * half, align_bytes=64) for half in range(2)
+        ]
         z_late = keep.tile([P, LATE_BLOCKS, 2, P, 2], BF16, align_bytes=64)
 
         def round_sums(rows, c, sums, copy, width=32):
@@ -257,12 +262,19 @@ def tile_picked_wlapl_gelu_l_kernel(
 
         early = {}
 
+        def early_parts(c, tile, half):
+            return [(2 * b + c % 2, tile[:, (2 * half + b) * P : (2 * half + b + 1) * P]) for b in range(2)]
+
         def early_open(c):
-            early[c] = bank(EARLY_SUM_BANKS[c])
-            add_turned(early[c], blocks_of(h[c][:], 4), True, False)
+            for half in range(2):
+                if c % 2 == 0:
+                    early[half, c // 2] = bank(EARLY_SUM_BANKS[2 * (c // 2) + half])
+                add_turned(early[half, c // 2], early_parts(c, h[c][:], half), c % 2 == 0, False)
 
         def early_term(c, d):
-            add_turned(early[c], blocks_of(fused(c, d, 0, BANK, minus_gate[d]), 4), False, d == LISTS - 1)
+            term = fused(c, d, 0, BANK, minus_gate[d])
+            for half in range(2):
+                add_turned(early[half, c // 2], early_parts(c, term, half), False, d == LISTS - 1 and c % 2 == 1)
 
         def late_open(pair):
             sums = bank(LATE_SUM_BANKS[pair])
@@ -274,19 +286,19 @@ def tile_picked_wlapl_gelu_l_kernel(
             return [(2 * b + c % 2, part) for b, part in blocks_of(tile, 2)]
 
         packed_first = head.tile([P, P, PACK], BF16, offset=3584, align_bytes=64)
-        w1_mx = [quantise_w1(0, nc.vector.tensor_copy, packed_first[:])]
+        w1_mx = [quantise_w1(0, round_w1(0, nc.vector.tensor_copy, packed_first[:]))]
         early_gates = head.tile([P, LISTS, BANK], F32, offset=0, align_bytes=64)
         for d in range(LISTS):
             negate_gate(d, spreads[d], early_gates[:, d, :])
         packed_second = head.tile([P, P, PACK], BF16, offset=4096, align_bytes=64)
-        w1_mx.append(quantise_w1(1, nc.vector.tensor_copy, packed_second[:]))
+        w1_mx.append(quantise_w1(1, round_w1(1, nc.vector.tensor_copy, packed_second[:])))
 
         def scalar_weights(c):
             if c == 2:
                 packed = ring.tile([P, P, PACK], BF16, name="w1_packed2", tag="w1_codes0", align_bytes=64)
             else:
                 packed = laid.tile([P, P, PACK], BF16, name="w1_packed3", offset=21760, align_bytes=64)
-            w1_mx.append(quantise_w1(c, nc.scalar.copy, packed[:]))
+            return round_w1(c, nc.scalar.copy, packed[:])
 
         plain = [
             laid.tile([P, LISTS, DEALT], F32, name=f"plain{c}", offset=(22784, 1024, 3072)[c], align_bytes=64)
@@ -295,7 +307,7 @@ def tile_picked_wlapl_gelu_l_kernel(
         plain.append(keep.tile([P, LISTS, DEALT], F32, name="plain3"))
 
         gelu(0, first_product(0, *w1_mx[0]))
-        scalar_weights(2)
+        w1_mx.append(quantise_w1(2, scalar_weights(2)))
         gelu(1, first_product(1, *w1_mx[1]))
         early_open(0)
         pre2 = first_product(2, *w1_mx[2])
@@ -307,42 +319,55 @@ def tile_picked_wlapl_gelu_l_kernel(
                 nc.tensor.transpose(dealt_gate[:, d, j, :], dealt_cols[:, d, j : j + 1].to_broadcast([P, P]), ident[:])
         late = [late_open(0)]
         early_term(0, 1)
-        scalar_weights(3)
+        packed_last = scalar_weights(3)
         fetch(0, 0, T - DEALT, plain[0][:, 0, :])
         gelu(2, pre2)
         early_term(1, 0)
-        pre3 = first_product(3, *w1_mx[3])
+        early_open(2)
+        early_term(1, 1)
+        pre3 = first_product(3, *quantise_w1(3, packed_last))
         fetch(0, 1, T - DEALT, plain[0][:, 1, :])
         deal_plain(0)
         minus_late = laid.tile([P, FUSED], F32, offset=14336 - 1024, align_bytes=64)
         nc.scalar.activation(out=minus_late[:], in_=gate_late[:, 0, 0:FUSED], func=ACT.Copy, scale=-1.0)
-        gelu(3, pre3)
-        for c in range(1, TILES):
+
+        def fetch_dealt(c):
             for d in range(LISTS):
                 fetch(c, d, T - DEALT, plain[c][:, d, :])
             deal_plain(c)
-        early_open(2)
-        early_term(1, 1)
+
+        def late_term(c):
+            add_turned(late[c // 2], late_blocks(c, fused(c, 0, BANK, FUSED, minus_late[:])), False, False)
+
+        fetch_dealt(1)
+        gelu(3, pre3)
+        fetch_dealt(2)
+        fetch_dealt(3)
         early_term(2, 0)
+        early_term(2, 1)
         early_open(3)
         late = late + [late_open(1)]
-        early_term(2, 1)
+        late_term(0)
+        late_term(1)
         early_term(3, 0)
         early_term(3, 1)
-        for c in range(TILES):
-            add_turned(late[c // 2], late_blocks(c, fused(c, 0, BANK, FUSED, minus_late[:])), False, False)
+        late_term(2)
+        late_term(3)
         plain_late = laid.tile([P, TILES, FUSED], F32, offset=40960, align_bytes=64)
-        scaled_late = keep.tile([P, TILES, FUSED], F32)
+        scaled_late = laid.tile([P, TILES, FUSED], F32, offset=51200, align_bytes=64)
         for c in range(TILES):
             fetch(c, 1, BANK, plain_late[:, c, :])
             scale(scaled_late[:, c, :], plain_late[:, c, :], gate_late[:, 1, 0:FUSED])
             add_turned(late[c // 2], late_blocks(c, scaled_late[:, c, :]), False, c % 2 == 1)
-        for c in range(TILES):
-            round_sums(z_early, c, early[c], scalar_copy)
-        back_early = [turn_back(z_early, 2 * i, 2, bank(i)) for i in range(2)]
         for pair in range(2):
-            round_sums(z_late, pair, late[pair], scalar_copy, 64)
-        packed = [keep.tile([P, 2 * P, PACK], BF16, name=f"z_packed{i}", align_bytes=64) for i in range(4)]
+            for half in range(2):
+                round_sums(z_early[half][:], pair, early[half, pair], scalar_copy, 64)
+        back_early = [turn_back(z_early[half], 0, 2, bank(half)) for half in range(2)]
+        for pair in range(2):
+            round_sums(z_late[:], pair, late[pair], scalar_copy, 64)
+        packed = [
+            laid.tile([P, 2 * P, PACK], BF16, name=f"z_packed{i}", offset=51200 + 2048 * i, align_bytes=64) for i in range(4)
+        ]
         for i in range(2):
             interleave(packed[i], 0, 2, back_early[i], scalar_copy)
         interleave(packed[2], 0, 2, turn_back(z_late, 0, 2, bank(6)), scalar_copy)
@@ -380,12 +405,11 @@ def tile_picked_wlapl_gelu_l_kernel(
             )
 
         finish_dealt(0)
+        prods = {0: second_product(packed[0], 2 * P, bank(7, 2 * P), 6144)}
         finish_dealt(1)
-        prods = {
-            i: second_product(packed[i], 2 * P, bank(number, 2 * P), at)
-            for i, number, at in ((0, 7, 47104), (3, 4, 50176), (1, 3, 48128), (2, 5, 49152))
-        }
+        for i, number, at in ((1, 3, 47104), (3, 4, 50176), (2, 5, 49152)):
+            prods[i] = second_product(packed[i], 2 * P, bank(number, 2 * P), at)
         store(0, 2 * P, prods[0], scalar_copy, nc.sync)
-        store(6 * P, 2 * P, prods[3], scalar_copy, nc.sync)
-        store(2 * P, 2 * P, prods[1], vector_copy, nc.sync)
+        store(2 * P, 2 * P, prods[1], scalar_copy, nc.sync)
+        store(6 * P, 2 * P, prods[3], vector_copy, nc.sync)
         store(4 * P, 2 * P, prods[2], scalar_copy, nc.scalar)

@@ -26,7 +26,12 @@ LISTS = 2
 
 W1_LOADS = ((0, 128), (128, 128), (256, 128), (384, 128))
 SPREAD_BANKS = (6, 7)
-FIRST_BANKS = ((2, 3, 4, 5), (4, 5), (2, 3), (2, 3))
+FIRST_PIECES = (
+    ((2, 0, 256), (3, 256, 256), (4, 512, 256), (5, 768, 256)),
+    ((6, 0, 256), (7, 256, 256), (4, 512, 512)),
+    ((2, 0, 512), (3, 512, 512)),
+    ((2, 0, 512), (3, 512, 512)),
+)
 EARLY_SUM_BANKS = (0, 1, 6, 7)
 LATE_SUM_BANKS = (5, 2)
 DEALT_GATE_BANK = 4
@@ -56,7 +61,7 @@ def tile_picked_wlapl_gelu_l_kernel(
             tile = psum.tile([P, columns], F32, name=f"bank{number}", tag=f"bank{number}")
             return tile[:]
 
-        x_plane = laid.tile([P, T], U8, offset=16384, align_bytes=64)
+        x_plane = laid.tile([P, BANK], U8, offset=16384, align_bytes=64)
         w2_plane = keep.tile([P, N], U8, align_bytes=64)
         nc.gpsimd.memset(x_plane[:].bitcast(I32), 0)
         nc.vector.memset(w2_plane[:].bitcast(I32), 0)
@@ -81,16 +86,18 @@ def tile_picked_wlapl_gelu_l_kernel(
 
         nc.sync.dma_start(out=gate_cols[:], in_=gate[:, 0, 0:BANK].rearrange("d (n j) -> n d j", j=4))
         load_w1(0)
-        load_scale_rows(nc, x_plane, x_scales[0])
+        x_rows = x_scales[0].bitcast(I32).rearrange("r (half n) -> half r n", half=2)
+        for q in range(4):
+            nc.sync.dma_start(out=x_plane[32 * q : 32 * q + 8, :].bitcast(I32), in_=x_rows[:, 4 * q : 4 * q + 4, :])
         for half in range(2):
             half_bytes = x_bytes[:, PACK * BANK * half : PACK * BANK * (half + 1)]
             nc.sync.dma_start(out=x_codes[half][:].bitcast(I32), in_=half_bytes.bitcast(I32))
         load_w1(1)
         nc.sync.dma_start(lists[0][:], pos1)
         nc.sync.dma_start(lists[1][:], pos2)
-        nc.sync.dma_start(out=dealt_cols[:], in_=gate[:, 0, T - DEALT : T].rearrange("d (n j) -> n d j", j=2))
         load_w1(2)
         load_w1(3)
+        nc.sync.dma_start(out=dealt_cols[:], in_=gate[:, 0, T - DEALT : T].rearrange("d (n j) -> n d j", j=2))
         nc.sync.dma_start(out=gate_late[:], in_=gate[:, :, BANK : BANK + FUSED].rearrange("d q v -> q d v"))
         nc.sync.dma_start(out=w2_codes[:].bitcast(I32), in_=w2_words[0].rearrange("p n t -> p (n t)").bitcast(I32))
         load_scale_rows(nc, w2_plane, w2_scales[0])
@@ -144,17 +151,16 @@ def tile_picked_wlapl_gelu_l_kernel(
         h = [keep.tile([P, T], F32, name=f"h{c}") for c in range(TILES)]
 
         def first_product(c, codes, plane):
-            width = BANK // 2 if c == 0 else BANK
             pres = []
-            for at in range(0, T, width):
+            for number, at, width in FIRST_PIECES[c]:
                 cols = slice(at, at + width)
-                pre = bank(FIRST_BANKS[c][at // width], width)
+                pre = bank(number, width)
                 nc.tensor.matmul_mx(
                     out=pre,
                     lhsT=codes[:].bitcast(FP8X4),
                     lhsT_scale=plane[:],
                     rhs=x_codes[at // BANK][:, at % BANK : at % BANK + width].bitcast(FP8X4),
-                    rhs_scale=x_plane[:, cols],
+                    rhs_scale=x_plane[4 * (at // BANK) :, at % BANK : at % BANK + width],
                     start=True,
                     stop=True,
                 )

@@ -38,6 +38,7 @@ DEALT_GATE_BANK = 4
 FUSED = 256
 TERM_AT = {(0, 1, 0): 26624}
 DEALT = 256
+SHARED = 96
 LATE_BLOCKS = 2
 
 
@@ -383,7 +384,8 @@ def tile_picked_wlapl_gelu_l_kernel(
             for d in range(LISTS)
         ]
         less_first = [
-            laid.tile([P, PACK, P], F32, name=f"less_first{b}", offset=47104 + 2048 * b, align_bytes=64) for b in range(2)
+            laid.tile([P, PACK, n], F32, name=f"less_first{b}", offset=47104 + 1536 * b, align_bytes=64)
+            for b, n in enumerate((SHARED, DEALT - SHARED))
         ]
 
         def dealt_product(d, n0, n1):
@@ -395,14 +397,14 @@ def tile_picked_wlapl_gelu_l_kernel(
                 MULT,
             )
 
-        dealt_product(0, 0, 64)
-        nc.gpsimd.tensor_tensor(less_first[0][:], dealt_h[:, :, 0:P], dealt_terms[0][:, :, 0:P], SUBTRACT)
-        dealt_product(0, 64, P)
+        dealt_product(0, 0, SHARED // 2)
+        nc.gpsimd.tensor_tensor(less_first[0][:], dealt_h[:, :, :SHARED], dealt_terms[0][:, :, :SHARED], SUBTRACT)
+        dealt_product(0, SHARED // 2, P)
         dealt_product(1, 0, P)
-        nc.vector.tensor_tensor(less_first[1][:], dealt_h[:, :, P:], dealt_terms[0][:, :, P:], SUBTRACT)
+        nc.vector.tensor_tensor(less_first[1][:], dealt_h[:, :, SHARED:], dealt_terms[0][:, :, SHARED:], SUBTRACT)
 
         def finish_dealt(block):
-            cols = slice(block * P, (block + 1) * P)
+            cols = (slice(0, SHARED), slice(SHARED, DEALT))[block]
             nc.vector.tensor_tensor(
                 packed[3][:, cols, :].rearrange("p (m i) j -> p m j i", i=4),
                 less_first[block][:].rearrange("p j (m i) -> p m j i", i=4),

@@ -38,7 +38,8 @@ DEALT_GATE_BANK = 4
 FUSED = 256
 TERM_AT = {(0, 1, 0): 26624}
 DEALT = 256
-SHARED = 96
+LEAD = 48
+SHARED = 160
 LATE_BLOCKS = 2
 
 
@@ -362,10 +363,13 @@ def tile_picked_wlapl_gelu_l_kernel(
         late_term(3)
         plain_late = laid.tile([P, TILES, FUSED], F32, offset=40960, align_bytes=64)
         scaled_late = laid.tile([P, TILES, FUSED], F32, offset=51200, align_bytes=64)
-        for c in range(TILES):
-            fetch(c, 1, BANK, plain_late[:, c, :])
-            scale(scaled_late[:, c, :], plain_late[:, c, :], gate_late[:, 1, 0:FUSED])
-            add_turned(late[c // 2], late_blocks(c, scaled_late[:, c, :]), False, c % 2 == 1)
+        for pair in range(2):
+            tiles = slice(2 * pair, 2 * pair + 2)
+            for c in range(TILES)[tiles]:
+                fetch(c, 1, BANK, plain_late[:, c, :])
+            scale(scaled_late[:, tiles, :], plain_late[:, tiles, :], gate_late[:, 1:2, :].to_broadcast([P, 2, FUSED]))
+            for c in range(TILES)[tiles]:
+                add_turned(late[pair], late_blocks(c, scaled_late[:, c, :]), False, c % 2 == 1)
         for pair in range(2):
             for half in range(2):
                 round_sums(z_early[half][:], pair, early[half, pair], scalar_copy, 64)
@@ -384,7 +388,7 @@ def tile_picked_wlapl_gelu_l_kernel(
             for d in range(LISTS)
         ]
         less_first = [
-            laid.tile([P, PACK, n], F32, name=f"less_first{b}", offset=47104 + 1536 * b, align_bytes=64)
+            laid.tile([P, PACK, n], F32, name=f"less_first{b}", offset=47104 + 2560 * b, align_bytes=64)
             for b, n in enumerate((SHARED, DEALT - SHARED))
         ]
 
@@ -397,8 +401,9 @@ def tile_picked_wlapl_gelu_l_kernel(
                 MULT,
             )
 
-        dealt_product(0, 0, SHARED // 2)
-        nc.gpsimd.tensor_tensor(less_first[0][:], dealt_h[:, :, :SHARED], dealt_terms[0][:, :, :SHARED], SUBTRACT)
+        for v0, v1 in ((0, LEAD), (LEAD, SHARED)):
+            dealt_product(0, v0 // 2, v1 // 2)
+            nc.gpsimd.tensor_tensor(less_first[0][:, :, v0:v1], dealt_h[:, :, v0:v1], dealt_terms[0][:, :, v0:v1], SUBTRACT)
         dealt_product(0, SHARED // 2, P)
         dealt_product(1, 0, P)
         nc.vector.tensor_tensor(less_first[1][:], dealt_h[:, :, SHARED:], dealt_terms[0][:, :, SHARED:], SUBTRACT)
@@ -415,7 +420,7 @@ def tile_picked_wlapl_gelu_l_kernel(
         finish_dealt(0)
         prods = {0: second_product(packed[0], 2 * P, bank(7, 2 * P), 6144)}
         finish_dealt(1)
-        for i, number, at in ((1, 3, 47104), (3, 4, 50176), (2, 5, 49152)):
+        for i, number, at in ((1, 3, 47104), (3, 4, 48128), (2, 5, 49664)):
             prods[i] = second_product(packed[i], 2 * P, bank(number, 2 * P), at)
         store(0, 2 * P, prods[0], scalar_copy, nc.sync)
         store(2 * P, 2 * P, prods[1], scalar_copy, nc.sync)

@@ -39,7 +39,7 @@ FUSED = 256
 TERM_AT = {(0, 1, 0): 26624}
 DEALT = 256
 LEAD = 48
-SHARED = 160
+SHARED = 152
 LATE_BLOCKS = 2
 
 
@@ -363,13 +363,10 @@ def tile_picked_wlapl_gelu_l_kernel(
         late_term(3)
         plain_late = laid.tile([P, TILES, FUSED], F32, offset=40960, align_bytes=64)
         scaled_late = laid.tile([P, TILES, FUSED], F32, offset=51200, align_bytes=64)
-        for pair in range(2):
-            tiles = slice(2 * pair, 2 * pair + 2)
-            for c in range(TILES)[tiles]:
-                fetch(c, 1, BANK, plain_late[:, c, :])
-            scale(scaled_late[:, tiles, :], plain_late[:, tiles, :], gate_late[:, 1:2, :].to_broadcast([P, 2, FUSED]))
-            for c in range(TILES)[tiles]:
-                add_turned(late[pair], late_blocks(c, scaled_late[:, c, :]), False, c % 2 == 1)
+        for c in range(TILES):
+            fetch(c, 1, BANK, plain_late[:, c, :])
+            scale(scaled_late[:, c, :], plain_late[:, c, :], gate_late[:, 1, 0:FUSED])
+            add_turned(late[c // 2], late_blocks(c, scaled_late[:, c, :]), False, c % 2 == 1)
         for pair in range(2):
             for half in range(2):
                 round_sums(z_early[half][:], pair, early[half, pair], scalar_copy, 64)
@@ -388,7 +385,7 @@ def tile_picked_wlapl_gelu_l_kernel(
             for d in range(LISTS)
         ]
         less_first = [
-            laid.tile([P, PACK, n], F32, name=f"less_first{b}", offset=47104 + 2560 * b, align_bytes=64)
+            laid.tile([P, PACK, n], F32, name=f"less_first{b}", offset=47104 + 2432 * b, align_bytes=64)
             for b, n in enumerate((SHARED, DEALT - SHARED))
         ]
 
@@ -420,7 +417,7 @@ def tile_picked_wlapl_gelu_l_kernel(
         finish_dealt(0)
         prods = {0: second_product(packed[0], 2 * P, bank(7, 2 * P), 6144)}
         finish_dealt(1)
-        for i, number, at in ((1, 3, 47104), (3, 4, 48128), (2, 5, 49664)):
+        for i, number, at in ((1, 3, 47104), (3, 4, 48128), (2, 5, 49536)):
             prods[i] = second_product(packed[i], 2 * P, bank(number, 2 * P), at)
         store(0, 2 * P, prods[0], scalar_copy, nc.sync)
         store(2 * P, 2 * P, prods[1], scalar_copy, nc.sync)

from contextlib import ExitStack

import concourse.mybir as mybir
from concourse.masks import make_identity

K, T, H, N = 512, 1024, 512, 128
FLOPS = 2 * K * H * T + 2 * H * N * T

F32 = mybir.dt.float32
BF16 = mybir.dt.bfloat16
I32 = mybir.dt.int32
U32 = mybir.dt.uint32
U16 = mybir.dt.uint16
U8 = mybir.dt.uint8
FP8X4 = mybir.dt.float8_e4m3fn_x4
ACT = mybir.ActivationFunctionType
MULT = mybir.AluOpType.mult
SUBTRACT = mybir.AluOpType.subtract

P = 128
PACK = 4
BANK = 512
LANES = 16
TILES = H // P
LISTS = 2

W1_LOADS = ((0, 128), (128, 128), (256, 128), (384, 128))
SPREAD_BANKS = (6, 7)
FIRST_PIECES = (
    ((2, 0, 256), (3, 256, 256), (4, 512, 256), (5, 768, 256)),
    ((6, 0, 256), (7, 256, 256), (4, 512, 512)),
    ((2, 0, 512), (3, 512, 512)),
    ((2, 0, 512), (3, 512, 512)),
)
EARLY_SUM_BANKS = (0, 1, 6, 7)
LATE_SUM_BANKS = (5, 2)
DEALT_GATE_BANK = 4
FUSED = 256
TERM_AT = {(0, 1, 0): 26624}
DEALT = 256
LEAD = 48
SHARED = 152
LATE_BLOCKS = 2


def load_scale_rows(nc, plane, rows):
    for q in range(4):
        nc.sync.dma_start(out=plane[32 * q : 32 * q + 4, :].bitcast(I32), in_=rows[4 * q : 4 * q + 4, :].bitcast(I32))


def tile_picked_wlapl_gelu_l_kernel(
    tc, x_words, x_scales, w1, w2_words, w2_scales, gate, pos1, pos2, out
):
    nc = tc.nc
    with ExitStack() as ctx:
        keep = ctx.enter_context(tc.tile_pool(name="keep", bufs=1))
        ring = ctx.enter_context(tc.tile_pool(name="ring", bufs=1))
        head = ctx.enter_context(tc.tile_pool(name="head", bufs=1))
        laid = ctx.enter_context(tc.tile_pool(name="laid", bufs=1))
        psum = ctx.enter_context(tc.psum_pool(name="psum", bufs=1))

        def bank(number, columns=BANK):
            tile = psum.tile([P, columns], F32, name=f"bank{number}", tag=f"bank{number}")
            return tile[:]

        x_plane = laid.tile([P, BANK], U8, offset=16384, align_bytes=64)
        w2_plane = keep.tile([P, N], U8, align_bytes=64)
        nc.gpsimd.memset(x_plane[:].bitcast(I32), 0)
        nc.vector.memset(w2_plane[:].bitcast(I32), 0)

        w1_rows = w1.rearrange("(p j) c -> p j c", j=PACK)
        w1_loaded = [ring.tile([P, PACK, P], F32, name=f"w1_loaded{c}", align_bytes=64) for c in range(2)]
        w1_loaded = w1_loaded + [
            laid.tile([P, PACK, P], F32, name=f"w1_loaded{c}", offset=26624 + 2048 * (c - 2), align_bytes=64) for c in (2, 3)
        ]
        w1_raw = [tile[:] for tile in w1_loaded]
        x_codes = [laid.tile([P, BANK], U32, name=f"x_codes{half}", offset=45056 - 2048 * half, align_bytes=64) for half in range(2)]
        x_bytes = x_words[0].rearrange("p n t -> p (n t)")
        gate_cols = keep.tile([P, LISTS, 4], F32)
        gate_late = keep.tile([P, LISTS, FUSED], F32)
        dealt_cols = keep.tile([P, LISTS, 2], F32)
        lists = [keep.tile([P, T // LANES], U16, name=f"list{d}") for d in range(LISTS)]
        w2_codes = keep.tile([P, N], U32, align_bytes=64)

        def load_w1(i):
            first, cols = W1_LOADS[i]
            nc.sync.dma_start(out=w1_loaded[i][:], in_=w1_rows[:, :, first : first + cols])

        nc.sync.dma_start(out=gate_cols[:], in_=gate[:, 0, 0:BANK].rearrange("d (n j) -> n d j", j=4))
        load_w1(0)
        x_rows = x_scales[0].bitcast(I32).rearrange("r (half n) -> half r n", half=2)
        for q in range(4):
            nc.sync.dma_start(out=x_plane[32 * q : 32 * q + 8, :].bitcast(I32), in_=x_rows[:, 4 * q : 4 * q + 4, :])
        for half in range(2):
            half_bytes = x_bytes[:, PACK * BANK * half : PACK * BANK * (half + 1)]
            nc.sync.dma_start(out=x_codes[half][:].bitcast(I32), in_=half_bytes.bitcast(I32))
        load_w1(1)
        nc.sync.dma_start(lists[0][:], pos1)
        nc.sync.dma_start(lists[1][:], pos2)
        load_w1(2)
        load_w1(3)
        nc.sync.dma_start(out=dealt_cols[:], in_=gate[:, 0, T - DEALT : T].rearrange("d (n j) -> n d j", j=2))
        nc.sync.dma_start(out=gate_late[:], in_=gate[:, :, BANK : BANK + FUSED].rearrange("d q v -> q d v"))
        nc.sync.dma_start(out=w2_codes[:].bitcast(I32), in_=w2_words[0].rearrange("p n t -> p (n t)").bitcast(I32))
        load_scale_rows(nc, w2_plane, w2_scales[0])

        first_ident = ring.tile([P, P], F32, tag="w1_codes0", align_bytes=64)
        make_identity(nc, first_ident[:])
        ident = keep.tile([P, P], F32)
        make_identity(nc, ident[:])

        minus_gate = []

        def spread_gate(d):
            spread = bank(SPREAD_BANKS[d]).rearrange("q (j n) -> q j n", j=4)
            for j in range(4):
                nc.tensor.transpose(spread[:, j, :], gate_cols[:, d, j : j + 1].to_broadcast([P, P]), (first_ident, ident)[d][:])
            return spread

        def negate_gate(d, spread, tile):
            minus_gate.append(tile)
            nc.vector.tensor_scalar(
                out=tile.rearrange("q (n j) -> q n j", j=4),
                in0=spread.rearrange("q j n -> q n j"),
                scalar1=-1.0,
                scalar2=None,
                op0=MULT,
            )

        spreads = [spread_gate(d) for d in range(LISTS)]

        def round_w1(c, copy, packed):
            copy(
                out=packed.rearrange("p (m i) j -> p m j i", i=4),
                in_=w1_raw[c].rearrange("p j (m i) -> p m j i", i=4),
            )
            return packed

        def quantise_w1(c, packed):
            if c > 0:
                codes = laid.tile([P, P], U32, name=f"w1_codes{c}", offset={1: 22528, 2: 1024, 3: 3072}[c], align_bytes=64)
            else:
                codes = ring.tile([P, P], U32, name=f"w1_codes{c}", tag=f"w1_codes{c}", align_bytes=64)
            if c >= 2:
                plane = laid.tile([P, P], U8, name=f"w1_plane{c}", offset=14336 + P * (c - 3), align_bytes=64)
            else:
                plane = keep.tile([P, P], U8, name=f"w1_plane{c}", align_bytes=64)
            nc.vector.quantize_mx(
                out=codes[:].bitcast(FP8X4), scales=plane[:], in_=packed.rearrange("p m j -> p (m j)")
            )
            return codes, plane

        h = [keep.tile([P, T], F32, name=f"h{c}") for c in range(TILES)]

        def first_product(c, codes, plane):
            pres = []
            for number, at, width in FIRST_PIECES[c]:
                cols = slice(at, at + width)
                pre = bank(number, width)
                nc.tensor.matmul_mx(
                    out=pre,
                    lhsT=codes[:].bitcast(FP8X4),
                    lhsT_scale=plane[:],
                    rhs=x_codes[at // BANK][:, at % BANK : at % BANK + width].bitcast(FP8X4),
                    rhs_scale=x_plane[4 * (at // BANK) :, at % BANK : at % BANK + width],
                    start=True,
                    stop=True,
                )
                pres.append((cols, pre))
            return pres

        def gelu(c, pres):
            for cols, pre in pres:
                nc.scalar.activation(out=h[c][:, cols], in_=pre, func=ACT.Gelu_apprx_tanh)
            deal_h(c)

        def gathered(c, d, v0, n):
            return h[c][:].indirect(lists[d][:, v0 // LANES : (v0 + n) // LANES])

        dealt_h = keep.tile([P, PACK, DEALT], F32)
        dealt_plain = laid.tile([P, PACK, LISTS, DEALT], F32, offset=32768, align_bytes=64)

        def fetch(c, d, v0, plain):
            nc.scalar.activation(out=plain, in_=gathered(c, d, v0, DEALT), func=ACT.Copy)

        def scale(scaled, plain, gates):
            nc.vector.scalar_tensor_tensor(out=scaled, in0=plain, scalar=-1.0, in1=gates, op0=MULT, op1=MULT)

        def deal_plain(c):
            for t in range(PACK):
                nc.sync.dma_start(out=dealt_plain[32 * c : 32 * c + 32, t, :, :], in_=plain[c][t:P:PACK])

        def deal_h(c):
            for t in range(PACK):
                nc.sync.dma_start(out=dealt_h[32 * c : 32 * c + 32, t, :], in_=h[c][t:P:PACK, T - DEALT : T])

        def fused(c, d, v0, n, gates):
            if (c, d, v0) in TERM_AT:
                term = laid.tile([P, n], F32, name=f"term{c}_{d}_{v0}", offset=TERM_AT[(c, d, v0)], align_bytes=64)
            else:
                term = keep.tile([P, n], F32, name=f"term{c}_{d}_{v0}")
            nc.vector.tensor_tensor(term[:], gathered(c, d, v0, n), gates, MULT)
            return term[:]

        def add_turned(sums, parts, first, last):
            for k, (b, part) in enumerate(parts):
                nc.tensor.matmul(
                    sums[:, b * P : (b + 1) * P],
                    lhsT=part,
                    rhs=ident[:],
                    start=(first and k == 0),
                    stop=(last and k == len(parts) - 1),
                    is_transpose=True,
                )

        def blocks_of(tile, count, first=0):
            return [(b, tile[:, (first + b) * P : (first + b + 1) * P]) for b in range(count)]

        z_early = [
            laid.tile([P, 2, 2, P, 2], BF16, name=f"z_early{half}", offset=14336 + 2048 * half, align_bytes=64) for half in range(2)
        ]
        z_late = keep.tile([P, LATE_BLOCKS, 2, P, 2], BF16, align_bytes=64)

        def round_sums(rows, c, sums, copy, width=32):
            copy(out=rows[:, :, :, width * c : width * (c + 1), :], in_=sums.rearrange("v (b p u e) -> v b u p e", p=width, u=2, e=2))

        def turn_back(rows, b0, nb, back):
            pairs = rows[:].rearrange("v b u p e -> v (b u p e)").bitcast(F32)
            back = back.rearrange("p (b u v) -> p b u v", b=nb, u=2)
            for b in range(nb):
                for u in range(2):
                    at = (2 * (b0 + b) + u) * P
                    nc.tensor.transpose(back[:, b, u, :], pairs[:, at : at + P], ident[:])
            return back

        def interleave(z_packed, b0, nb, back, copy):
            z_words = z_packed[:].rearrange("p v t -> p (v t)").bitcast(F32)
            copy(
                out=z_words[:, 2 * P * b0 : 2 * P * (b0 + nb)].rearrange("p (b v u) -> p b v u", b=nb, u=2),
                in_=back.rearrange("p b u v -> p b v u"),
            )

        def quantise_z(z_packed, codes, plane):
            nc.vector.quantize_mx(out=codes.bitcast(FP8X4), scales=plane, in_=z_packed[:].rearrange("p v t -> p (v t)"))

        def project(z_codes, z_plane, prod):
            nc.tensor.matmul_mx(
                out=prod,
                lhsT=w2_codes[:].bitcast(FP8X4),
                lhsT_scale=w2_plane[:],
                rhs=z_codes[:].bitcast(FP8X4),
                rhs_scale=z_plane[:],
                start=True,
                stop=True,
            )
            return prod

        def second_product(z_packed, width, prod, at):
            z_codes = laid.tile([P, width], U32, name=f"z_codes{at}", offset=at, align_bytes=64)
            z_plane = keep.tile([P, width], U8, name=f"z_plane{at}", align_bytes=64)
            quantise_z(z_packed, z_codes[:], z_plane[:])
            return project(z_codes, z_plane, prod)

        def store(v0, width, prod, copy, queue):
            result = keep.tile([P, width], F32, name=f"result{v0}")
            copy(out=result[:], in_=prod)
            queue.dma_start(out=out[:, v0 : v0 + width], in_=result[:])

        scalar_copy, vector_copy = nc.scalar.copy, nc.vector.tensor_copy

        early = {}

        def early_parts(c, tile, half):
            return [(2 * b + c % 2, tile[:, (2 * half + b) * P : (2 * half + b + 1) * P]) for b in range(2)]

        def early_open(c):
            for half in range(2):
                if c % 2 == 0:
                    early[half, c // 2] = bank(EARLY_SUM_BANKS[2 * (c // 2) + half])
                add_turned(early[half, c // 2], early_parts(c, h[c][:], half), c % 2 == 0, False)

        def early_term(c, d):
            term = fused(c, d, 0, BANK, minus_gate[d])
            for half in range(2):
                add_turned(early[half, c // 2], early_parts(c, term, half), False, d == LISTS - 1 and c % 2 == 1)

        def late_open(pair):
            sums = bank(LATE_SUM_BANKS[pair])
            parts = [(2 * b + c % 2, h[c][:, BANK + b * P : BANK + (b + 1) * P]) for c in (2 * pair, 2 * pair + 1) for b in range(2)]
            add_turned(sums, parts, True, False)
            return sums

        def late_blocks(c, tile):
            return [(2 * b + c % 2, part) for b, part in blocks_of(tile, 2)]

        packed_first = head.tile([P, P, PACK], BF16, offset=3584, align_bytes=64)
        w1_mx = [quantise_w1(0, round_w1(0, nc.vector.tensor_copy, packed_first[:]))]
        early_gates = head.tile([P, LISTS, BANK], F32, offset=0, align_bytes=64)
        for d in range(LISTS):
            negate_gate(d, spreads[d], early_gates[:, d, :])
        packed_second = head.tile([P, P, PACK], BF16, offset=4096, align_bytes=64)
        w1_mx.append(quantise_w1(1, round_w1(1, nc.vector.tensor_copy, packed_second[:])))

        def scalar_weights(c):
            if c == 2:
                packed = ring.tile([P, P, PACK], BF16, name="w1_packed2", tag="w1_codes0", align_bytes=64)
            else:
                packed = laid.tile([P, P, PACK], BF16, name="w1_packed3", offset=21760, align_bytes=64)
            return round_w1(c, nc.scalar.copy, packed[:])

        plain = [
            laid.tile([P, LISTS, DEALT], F32, name=f"plain{c}", offset=(22784, 1024, 3072)[c], align_bytes=64)
            for c in range(3)
        ]
        plain.append(keep.tile([P, LISTS, DEALT], F32, name="plain3"))

        gelu(0, first_product(0, *w1_mx[0]))
        w1_mx.append(quantise_w1(2, scalar_weights(2)))
        gelu(1, first_product(1, *w1_mx[1]))
        early_open(0)
        pre2 = first_product(2, *w1_mx[2])
        early_term(0, 0)
        early_open(1)
        dealt_gate = bank(DEALT_GATE_BANK).rearrange("q (d j n) -> q d j n", d=LISTS, j=2)
        for d in range(LISTS):
            for j in range(2):
                nc.tensor.transpose(dealt_gate[:, d, j, :], dealt_cols[:, d, j : j + 1].to_broadcast([P, P]), ident[:])
        late = [late_open(0)]
        early_term(0, 1)
        packed_last = scalar_weights(3)
        fetch(0, 0, T - DEALT, plain[0][:, 0, :])
        gelu(2, pre2)
        early_term(1, 0)
        early_open(2)
        early_term(1, 1)
        pre3 = first_product(3, *quantise_w1(3, packed_last))
        fetch(0, 1, T - DEALT, plain[0][:, 1, :])
        deal_plain(0)
        minus_late = laid.tile([P, FUSED], F32, offset=14336 - 1024, align_bytes=64)
        nc.scalar.activation(out=minus_late[:], in_=gate_late[:, 0, 0:FUSED], func=ACT.Copy, scale=-1.0)

        def fetch_dealt(c):
            for d in range(LISTS):
                fetch(c, d, T - DEALT, plain[c][:, d, :])
            deal_plain(c)

        def late_term(c):
            add_turned(late[c // 2], late_blocks(c, fused(c, 0, BANK, FUSED, minus_late[:])), False, False)

        fetch_dealt(1)
        gelu(3, pre3)
        fetch_dealt(2)
        fetch_dealt(3)
        early_term(2, 0)
        early_term(2, 1)
        early_open(3)
        late = late + [late_open(1)]
        late_term(0)
        late_term(1)
        early_term(3, 0)
        early_term(3, 1)
        late_term(2)
        late_term(3)
        plain_late = laid.tile([P, TILES, FUSED], F32, offset=40960, align_bytes=64)
        scaled_late = laid.tile([P, TILES, FUSED], F32, offset=51200, align_bytes=64)
        for c in range(TILES):
            fetch(c, 1, BANK, plain_late[:, c, :])
            scale(scaled_late[:, c, :], plain_late[:, c, :], gate_late[:, 1, 0:FUSED])
            add_turned(late[c // 2], late_blocks(c, scaled_late[:, c, :]), False, c % 2 == 1)
        for pair in range(2):
            for half in range(2):
                round_sums(z_early[half][:], pair, early[half, pair], scalar_copy, 64)
        back_early = [turn_back(z_early[half], 0, 2, bank(half)) for half in range(2)]
        for pair in range(2):
            round_sums(z_late[:], pair, late[pair], scalar_copy, 64)
        packed = [
            laid.tile([P, 2 * P, PACK], BF16, name=f"z_packed{i}", offset=51200 + 2048 * i, align_bytes=64) for i in range(4)
        ]
        for i in range(2):
            interleave(packed[i], 0, 2, back_early[i], scalar_copy)
        interleave(packed[2], 0, 2, turn_back(z_late, 0, 2, bank(6)), scalar_copy)

        dealt_terms = [
            laid.tile([P, PACK, DEALT], F32, name=f"dealt_term{d}", offset=(6144, 18432)[d], align_bytes=64)
            for d in range(LISTS)
        ]
        less_first = [
            laid.tile([P, PACK, n], F32, name=f"less_first{b}", offset=47104 + 2432 * b, align_bytes=64)
            for b, n in enumerate((SHARED, DEALT - SHARED))
        ]

        def dealt_product(d, n0, n1):
            gates = dealt_gate[:, d, :, n0:n1].rearrange("q j n -> q n j").unsqueeze(1).to_broadcast([P, PACK, n1 - n0, 2])
            nc.vector.tensor_tensor(
                dealt_terms[d][:, :, 2 * n0 : 2 * n1].rearrange("p t (n j) -> p t n j", j=2),
                dealt_plain[:, :, d, 2 * n0 : 2 * n1].rearrange("p t (n j) -> p t n j", j=2),
                gates,
                MULT,
            )

        for v0, v1 in ((0, LEAD), (LEAD, SHARED)):
            dealt_product(0, v0 // 2, v1 // 2)
            nc.gpsimd.tensor_tensor(less_first[0][:, :, v0:v1], dealt_h[:, :, v0:v1], dealt_terms[0][:, :, v0:v1], SUBTRACT)
        dealt_product(0, SHARED // 2, P)
        dealt_product(1, 0, P)
        nc.vector.tensor_tensor(less_first[1][:], dealt_h[:, :, SHARED:], dealt_terms[0][:, :, SHARED:], SUBTRACT)

        def finish_dealt(block):
            cols = (slice(0, SHARED), slice(SHARED, DEALT))[block]
            nc.vector.tensor_tensor(
                packed[3][:, cols, :].rearrange("p (m i) j -> p m j i", i=4),
                less_first[block][:].rearrange("p j (m i) -> p m j i", i=4),
                dealt_terms[1][:, :, cols].rearrange("p j (m i) -> p m j i", i=4),
                SUBTRACT,
            )

        finish_dealt(0)
        prods = {0: second_product(packed[0], 2 * P, bank(7, 2 * P), 6144)}
        finish_dealt(1)
        for i, number, at in ((1, 3, 47104), (3, 4, 48128), (2, 5, 49536)):
            prods[i] = second_product(packed[i], 2 * P, bank(number, 2 * P), at)
        store(0, 2 * P, prods[0], scalar_copy, nc.sync)
        store(2 * P, 2 * P, prods[1], scalar_copy, nc.sync)
        store(6 * P, 2 * P, prods[3], vector_copy, nc.sync)
        store(4 * P, 2 * P, prods[2], scalar_copy, nc.scalar)
